import numpy as np
import ml_dtypes


def mxq(x, axis, fmt="e4m3"):
    dtype, down = {"e4m3": (ml_dtypes.float8_e4m3fn, 7), "e5m2": (ml_dtypes.float8_e5m2, 14)}[fmt]
    v = np.moveaxis(np.asarray(x, np.float32).astype(ml_dtypes.bfloat16).astype(np.float64), axis, -1)
    blocks = v.reshape(v.shape[:-1] + (-1, 32))
    amax = np.abs(blocks).max(-1, keepdims=True)
    byte = np.maximum(np.where(amax > 0, np.frexp(amax)[1] - 1 + 127, 0) - down, 1)
    scale = np.exp2(byte - 127.0)
    codes = (blocks / scale).astype(np.float32).astype(dtype).astype(np.float64)
    return np.moveaxis((codes * scale).reshape(v.shape), -1, axis)


WIDE = False


def mx_kscale(k):
    if not WIDE:
        return np.ones(k)
    levels = np.array([10, -10, 5, -5, 0])
    if k % 512:
        return np.exp2(np.random.permutation(np.resize(levels, k // 32))).repeat(32)
    a = np.empty((k // 512, 16))
    for p in range(k // 512):
        a[p, :8] = np.random.permutation(np.resize(levels, 8))
        for g in range(8):
            far = levels[np.abs(levels - a[p, g]) >= 10]
            a[p, g + 8] = far[np.random.randint(len(far))]
    return np.exp2(a.ravel()).repeat(32)


def f64(x):
    return np.asarray(x).astype(np.float64)


def striped(idx):
    return np.tile(np.asarray(idx).reshape(-1, 16).T, (8, 1)).astype(np.uint16)


def unstriped(offs):
    return offs[:16].T.reshape(-1).astype(np.int64)


E2M1 = np.array([0.0, 0.5, 1.0, 1.5, 2.0, 3.0, 4.0, 6.0, -0.0, -0.5, -1.0, -1.5, -2.0, -3.0, -4.0, -6.0])


def pack_weight(w, fmt):
    k, n = w.shape
    w = f64(np.asarray(w, np.float32).astype(ml_dtypes.bfloat16)).reshape(k // 32, 32, n)
    amax = np.abs(w).max(1)
    if fmt == "e4m3":
        byte = np.frexp(amax)[1] - 1 + 127 - 7
    else:
        mant, ex = np.frexp(amax / 6.0)
        byte = np.where(mant > 0.5, ex, ex - 1) + 127
    byte = np.clip(np.where(amax > 0, byte, 1), 1, 254)
    scaled = (w * np.exp2(127.0 - byte)[:, None, :]).reshape(k, n).astype(np.float32)
    by_word = np.ascontiguousarray(scaled.reshape(k // 512, 128, 4, n).transpose(0, 1, 3, 2))
    if fmt == "e4m3":
        words = by_word.astype(ml_dtypes.float8_e4m3fn).view(np.uint8)
    else:
        c = by_word.astype(ml_dtypes.float4_e2m1fn).view(np.uint8) & 0xF
        words = (c[..., 0::2] | (c[..., 1::2] << 4)).reshape(k // 512, 128, 2 * n)
    return np.ascontiguousarray(words), np.ascontiguousarray(byte.astype(np.uint8).reshape(k // 512, 16, n))


def unpack_weight(words, scales, fmt):
    g, _, n = scales.shape
    words = np.ascontiguousarray(words).reshape(g, 128, n, -1)
    if fmt == "e4m3":
        vals = words.view(ml_dtypes.float8_e4m3fn).astype(np.float64)
    else:
        nib = np.empty((g, 128, n, 4), np.uint8)
        nib[..., 0::2] = words & 0xF
        nib[..., 1::2] = words >> 4
        vals = E2M1[nib]
    vals = vals * np.repeat(np.exp2(scales.astype(np.float64) - 127.0), 8, axis=1)[..., None]
    return vals.transpose(0, 1, 3, 2).reshape(g * 512, n)


def sigmoid(v):
    return 1.0 / (1.0 + np.exp(-v))


B, N, T, D, NQ = 1, 512, 2048, 512, 256


def setup_inputs():
    n = np.random.standard_normal
    idx = np.random.permutation(T)[:B * N]
    idx2 = np.random.permutation(1024)[:B * N]
    s = mx_kscale(D)[:, None]
    kp = pack_weight(n((D, T)) / s, "e4m3")
    return {
        "qT": (n((B, D, NQ)) * s * (1.00 / np.sqrt(D))).astype(np.float32),
        "k_words": kp[0],
        "k_scales": kp[1],
        "cT": (n((D, 1024)) / s).astype(np.float32),
        "kb": np.tile(n(2048), (128, 1)).astype(np.float32),
        "offs": striped(idx),
        "offs2": striped(idx2),
    }


def reference(qT, k_words, k_scales, cT, kb, offs, offs2):
    idx = unstriped(offs)
    idx2 = unstriped(offs2)
    pick = lambda x, which: x[:, which].reshape(x.shape[0], B, -1).transpose(1, 0, 2)
    k = unpack_weight(k_words, k_scales, "e4m3")
    kg = pick(k, idx)
    cg = mxq(pick(f64(cT), idx2), 1, "e4m3")
    qq = mxq(f64(qT), 1, "e4m3")
    a = qq.transpose(0, 2, 1) @ kg
    z = qq.transpose(0, 2, 1) @ cg
    y = sigmoid(a + pick(f64(kb), idx)[:, :1, :] - z)
    return y

@@ -1,0 +1,197 @@
+from contextlib import ExitStack
+
+import concourse.mybir as mybir
+from concourse.masks import make_identity
+
+F32 = mybir.dt.float32
+BF16 = mybir.dt.bfloat16
+I32 = mybir.dt.int32
+U32 = mybir.dt.uint32
+U16 = mybir.dt.uint16
+U8 = mybir.dt.uint8
+FP8X4 = mybir.dt.float8_e4m3fn_x4
+ACT = mybir.ActivationFunctionType
+ALU = mybir.AluOpType
+
+P = 128
+D, NQ, N, T, T2 = 512, 256, 512, 2048, 1024
+HALF = N // 2
+FLOPS = 2 * 2 * NQ * N * D
+BYTES = 4 * D * NQ + D * T + 16 * T + 4 * D * T2 + 4 * T + 2 * 2 * P * (N // 16) + 4 * NQ * N
+
+
+def tile_attend_prefer_topk_kernel(tc, qT, k_words, k_scales, cT, kb, offs, offs2, out):
+    nc = tc.nc
+    with ExitStack() as ctx:
+        sb = ctx.enter_context(tc.tile_pool(name="sb", bufs=1))
+        ps = ctx.enter_context(tc.psum_pool(name="ps", bufs=1))
+
+        def tile(shape, dtype, name):
+            return sb.tile(shape, dtype, name=name, align_bytes=64)
+
+        list1 = tile([P, N // 16], U16, "list1")
+        list2 = tile([P, N // 16], U16, "list2")
+        kb_win = tile([P, T], F32, "kb_win")
+        ks_win = tile([P, T], U8, "ks_win")
+        kw_win = tile([P, T], I32, "kw_win")
+        q_raw = tile([P, 4, NQ], F32, "q_raw")
+        CH = [[(0, 512), (512, 1024)], [(0, 512), (512, 1024)]]
+        c_raw = [[tile([P, 2, b - a], F32, "c_raw%d_%d" % (u, a)) for a, b in CH[u]] for u in range(2)]
+        c_pair = [tile([P, T2, 2], BF16, "c_pair%d" % u) for u in range(2)]
+        warm = tile([P, 2], F32, "warm")
+        ident = tile([P, P], F32, "ident")
+
+        nc.vector.memset(warm[:, 0:1], 0.0)
+        nc.scalar.activation(out=warm[:, 1:2], in_=warm[:, 0:1], func=ACT.Sigmoid)
+        nc.vector.memset(kb_win[:].bitcast(I32), 0)
+        nc.gpsimd.memset(ks_win[:].bitcast(I32), 0)
+
+        c_rows = cT.rearrange("(p t) n -> p t n", t=4)
+
+        def load_c(u, i):
+            a, b = CH[u][i]
+            nc.sync.dma_start(out=c_raw[u][i][:], in_=c_rows[:, 2 * u : 2 * u + 2, a:b])
+
+        def load_q():
+            nc.sync.dma_start(out=q_raw[:], in_=qT[0].rearrange("(p t) n -> p t n", t=4))
+
+        def load_kw():
+            nc.sync.dma_start(out=kw_win[:], in_=k_words[0].rearrange("p n t -> p (n t)").bitcast(I32))
+
+        def load_kb(eng):
+            eng.dma_start(out=kb_win[0:1, :], in_=kb[0:1, :])
+
+        def load_ks(eng):
+            for r in range(4):
+                eng.dma_start(out=ks_win[r:P:32, :].bitcast(I32), in_=k_scales[0, r:16:4, :].bitcast(I32))
+
+        def load_lists():
+            nc.sync.dma_start(list1[:], offs)
+            nc.sync.dma_start(list2[:], offs2)
+
+        q_bf = tile([P, 2, NQ, 4], BF16, "q_bf")
+        q_codes = tile([P, 2 * NQ], U32, "q_codes")
+        q_scales = tile([P, 2 * NQ], U8, "q_scales")
+
+        def cast_q():
+            nc.vector.tensor_copy(out=q_bf[:, 0], in_=q_raw[:].rearrange("p t n -> p n t"))
+
+        def negate_q():
+            nc.vector.tensor_scalar(out=q_bf[:, 1], in0=q_bf[:, 0], scalar1=-1.0, scalar2=None, op0=ALU.mult)
+
+        def quant_q():
+            nc.vector.quantize_mx(out=q_codes[:].bitcast(FP8X4), scales=q_scales[:], in_=q_bf[:].rearrange("p s n t -> p (s n t)"))
+
+        def cast_c(u, i, eng="s", lo=None, hi=None):
+            a, b = CH[u][i]
+            lo = a if lo is None else lo
+            hi = b if hi is None else hi
+            src = c_raw[u][i][:, :, lo - a : hi - a].rearrange("p t n -> p n t")
+            if eng == "s":
+                nc.scalar.activation(out=c_pair[u][:, lo:hi, :], in_=src, func=ACT.Copy)
+            else:
+                nc.vector.tensor_copy(out=c_pair[u][:, lo:hi, :], in_=src)
+
+        kb_g = tile([P, N], F32, "kb_g")
+        kb_col = tile([P, 4], F32, "kb_col")
+        kb_all = tile([P, N], F32, "kb_all")
+        turn1 = ps.tile([P, N], F32, name="turn1")
+        turn2 = ps.tile([P, N], F32, name="turn2")
+
+        def gather_kb():
+            nc.vector.tensor_copy(out=kb_g[:], in_=kb_win[:].indirect(list1[:]))
+
+        def spread_kb():
+            for j in range(4):
+                nc.tensor.transpose(turn1[:, j * P : (j + 1) * P], kb_g[:, j * P : (j + 1) * P], ident[:])
+            nc.scalar.copy(out=kb_col[:], in_=turn1[:, 0:N:P])
+            for j in range(4):
+                nc.tensor.transpose(turn2[:, j * P : (j + 1) * P], kb_col[:, j : j + 1].to_broadcast([P, P]), ident[:])
+            nc.scalar.copy(out=kb_all[:], in_=turn2[:])
+
+        ks_g = tile([P, N], U8, "ks_g")
+        kw_g = [tile([P, HALF], U32, "kw_g%d" % h) for h in range(2)]
+        c_g = [tile([P, 2, HALF], U32, "c_g%d" % h) for h in range(2)]
+        c_w = [tile([P, HALF, 2], U32, "c_w%d" % h) for h in range(2)]
+        c_codes = [tile([P, HALF], U32, "c_codes%d" % h) for h in range(2)]
+        c_scales = [tile([P, HALF], U8, "c_scales%d" % h) for h in range(2)]
+        W = HALF // 16
+
+        def gather_ks():
+            nc.vector.tensor_copy(out=ks_g[:], in_=ks_win[:].indirect(list1[:]))
+
+        def gather_kw(h):
+            nc.vector.tensor_copy(out=kw_g[h][:], in_=kw_win[:].bitcast(U32).indirect(list1[:, h * W : (h + 1) * W]))
+
+        def gather_c(u, h):
+            win = c_pair[u][:].rearrange("p n t -> p (n t)").bitcast(U32)
+            nc.vector.tensor_copy(out=c_g[h][:, u, :], in_=win.indirect(list2[:, h * W : (h + 1) * W]))
+
+        def weave(h, eng="s"):
+            if eng == "s":
+                nc.scalar.copy(out=c_w[h][:], in_=c_g[h][:].rearrange("p u n -> p n u"))
+            else:
+                nc.vector.tensor_copy(out=c_w[h][:].rearrange("p n u -> p (n u)").bitcast(I32).rearrange("p (n u) -> p n u", u=2), in_=c_g[h][:].bitcast(I32).rearrange("p u n -> p n u"))
+
+        def quant_c(h):
+            nc.vector.quantize_mx(out=c_codes[h][:].bitcast(FP8X4), scales=c_scales[h][:], in_=c_w[h][:].rearrange("p n u -> p (n u)").bitcast(BF16))
+
+        acc = [[ps.tile([P, HALF], F32, name="acc%d%d" % (h, m)) for m in range(2)] for h in range(2)]
+        logit = [[tile([P, HALF], F32, "logit%d%d" % (h, m)) for m in range(2)] for h in range(2)]
+        prob = [[tile([P, HALF], F32, "prob%d%d" % (h, m)) for m in range(2)] for h in range(2)]
+
+        def mm_k(h, m, start):
+            rows = slice(m * P, (m + 1) * P)
+            nc.tensor.matmul_mx(out=acc[h][m][:], lhsT=q_codes[:, rows].bitcast(FP8X4), lhsT_scale=q_scales[:, rows],
+                                rhs=kw_g[h][:].bitcast(FP8X4), rhs_scale=ks_g[:, h * HALF : (h + 1) * HALF], start=start, stop=not start)
+
+        def mm_c(h, m, start):
+            rows = slice(NQ + m * P, NQ + (m + 1) * P)
+            nc.tensor.matmul_mx(out=acc[h][m][:], lhsT=q_codes[:, rows].bitcast(FP8X4), lhsT_scale=q_scales[:, rows],
+                                rhs=c_codes[h][:].bitcast(FP8X4), rhs_scale=c_scales[h][:], start=start, stop=not start)
+
+        def finish(h, m):
+            cols = slice(h * HALF, (h + 1) * HALF)
+            nc.vector.tensor_tensor(out=logit[h][m][:], in0=acc[h][m][:], in1=kb_all[:, cols], op=ALU.add)
+            nc.scalar.activation(out=prob[h][m][:], in_=logit[h][m][:], func=ACT.Sigmoid)
+            nc.sync.dma_start(out=out[0, m * P : (m + 1) * P, cols], in_=prob[h][m][:])
+
+        load_ks(nc.gpsimd)
+        make_identity(nc, ident[:])
+        load_kb(nc.scalar)
+        load_lists()
+        load_q()
+        load_c(0, 0)
+        load_c(0, 1)
+        load_c(1, 0)
+        load_c(1, 1)
+        load_kw()
+        cast_q()
+        negate_q()
+        cast_c(0, 0)
+        cast_c(0, 1)
+        gather_kb()
+        quant_q()
+        spread_kb()
+        cast_c(1, 0)
+        cast_c(1, 1)
+        gather_c(0, 0)
+        gather_c(0, 1)
+        gather_ks()
+        gather_c(1, 0)
+        weave(0)
+        gather_c(1, 1)
+        weave(1)
+        gather_kw(0)
+        quant_c(0)
+        for m in range(2):
+            mm_k(0, m, True)
+            mm_c(0, m, False)
+        gather_kw(1)
+        quant_c(1)
+        for m in range(2):
+            mm_k(1, m, True)
+            mm_c(1, m, False)
+        for h in range(2):
+            for m in range(2):
+                finish(h, m)

@@ -26,8 +26,8 @@ def tile_attend_prefer_topk_kernel(tc, qT, k_words, k_scales, cT, kb, offs, offs
         sb = ctx.enter_context(tc.tile_pool(name="sb", bufs=1))
         ps = ctx.enter_context(tc.psum_pool(name="ps", bufs=1))
 
-        def tile(shape, dtype, name):
-            return sb.tile(shape, dtype, name=name, align_bytes=64)
+        def tile(shape, dtype, name, tag=None):
+            return sb.tile(shape, dtype, name=name, tag=tag or name, align_bytes=64)
 
         list1 = tile([P, N // 16], U16, "list1")
         list2 = tile([P, N // 16], U16, "list2")
@@ -43,8 +43,9 @@ def tile_attend_prefer_topk_kernel(tc, qT, k_words, k_scales, cT, kb, offs, offs
 
         nc.vector.memset(warm[:, 0:1], 0.0)
         nc.scalar.activation(out=warm[:, 1:2], in_=warm[:, 0:1], func=ACT.Sigmoid)
-        nc.vector.memset(kb_win[:].bitcast(I32), 0)
+        nc.vector.memset(kb_win[:, 0:1024].bitcast(I32), 0)
         nc.gpsimd.memset(ks_win[:].bitcast(I32), 0)
+        nc.gpsimd.memset(kb_win[:, 1024:T].bitcast(I32), 0)
 
         c_rows = cT.rearrange("(p t) n -> p t n", t=4)
 
@@ -65,21 +66,17 @@ def tile_attend_prefer_topk_kernel(tc, qT, k_words, k_scales, cT, kb, offs, offs
             for r in range(4):
                 eng.dma_start(out=ks_win[r:P:32, :].bitcast(I32), in_=k_scales[0, r:16:4, :].bitcast(I32))
 
-        def load_lists():
-            nc.sync.dma_start(list1[:], offs)
-            nc.sync.dma_start(list2[:], offs2)
 
         q_bf = tile([P, 2, NQ, 4], BF16, "q_bf")
-        q_codes = tile([P, 2 * NQ], U32, "q_codes")
         q_scales = tile([P, 2 * NQ], U8, "q_scales")
 
         def cast_q():
-            nc.vector.tensor_copy(out=q_bf[:, 0], in_=q_raw[:].rearrange("p t n -> p n t"))
+            nc.scalar.copy(out=q_bf[:, 0], in_=q_raw[:].rearrange("p t n -> p n t"))
 
         def negate_q():
-            nc.vector.tensor_scalar(out=q_bf[:, 1], in0=q_bf[:, 0], scalar1=-1.0, scalar2=None, op0=ALU.mult)
+            nc.vector.tensor_scalar(out=q_bf[:, 1], in0=q_raw[:].rearrange("p t n -> p n t"), scalar1=-1.0, scalar2=None, op0=ALU.mult)
 
-        def quant_q():
+        def quant_q(q_codes):
             nc.vector.quantize_mx(out=q_codes[:].bitcast(FP8X4), scales=q_scales[:], in_=q_bf[:].rearrange("p s n t -> p (s n t)"))
 
         def cast_c(u, i, eng="s", lo=None, hi=None):
@@ -93,35 +90,34 @@ def tile_attend_prefer_topk_kernel(tc, qT, k_words, k_scales, cT, kb, offs, offs
                 nc.vector.tensor_copy(out=c_pair[u][:, lo:hi, :], in_=src)
 
         kb_g = tile([P, N], F32, "kb_g")
-        kb_col = tile([P, 4], F32, "kb_col")
-        kb_all = tile([P, N], F32, "kb_all")
         turn1 = ps.tile([P, N], F32, name="turn1")
         turn2 = ps.tile([P, N], F32, name="turn2")
 
         def gather_kb():
             nc.vector.tensor_copy(out=kb_g[:], in_=kb_win[:].indirect(list1[:]))
 
-        def spread_kb():
+        def turn_kb():
+            kb_col = tile([P, 4], F32, "kb_col", tag="c_raw1_512")
             for j in range(4):
                 nc.tensor.transpose(turn1[:, j * P : (j + 1) * P], kb_g[:, j * P : (j + 1) * P], ident[:])
             nc.scalar.copy(out=kb_col[:], in_=turn1[:, 0:N:P])
             for j in range(4):
                 nc.tensor.transpose(turn2[:, j * P : (j + 1) * P], kb_col[:, j : j + 1].to_broadcast([P, P]), ident[:])
+
+        def spread_kb():
             nc.scalar.copy(out=kb_all[:], in_=turn2[:])
 
         ks_g = tile([P, N], U8, "ks_g")
-        kw_g = [tile([P, HALF], U32, "kw_g%d" % h) for h in range(2)]
-        c_g = [tile([P, 2, HALF], U32, "c_g%d" % h) for h in range(2)]
+        kw_g = tile([P, N], U32, "kw_g")
         c_w = [tile([P, HALF, 2], U32, "c_w%d" % h) for h in range(2)]
-        c_codes = [tile([P, HALF], U32, "c_codes%d" % h) for h in range(2)]
         c_scales = [tile([P, HALF], U8, "c_scales%d" % h) for h in range(2)]
         W = HALF // 16
 
         def gather_ks():
             nc.vector.tensor_copy(out=ks_g[:], in_=ks_win[:].indirect(list1[:]))
 
-        def gather_kw(h):
-            nc.vector.tensor_copy(out=kw_g[h][:], in_=kw_win[:].bitcast(U32).indirect(list1[:, h * W : (h + 1) * W]))
+        def gather_kw():
+            nc.vector.tensor_copy(out=kw_g[:], in_=kw_win[:].bitcast(U32).indirect(list1[:]))
 
         def gather_c(u, h):
             win = c_pair[u][:].rearrange("p n t -> p (n t)").bitcast(U32)
@@ -134,7 +130,7 @@ def tile_attend_prefer_topk_kernel(tc, qT, k_words, k_scales, cT, kb, offs, offs
                 nc.vector.tensor_copy(out=c_w[h][:].rearrange("p n u -> p (n u)").bitcast(I32).rearrange("p (n u) -> p n u", u=2), in_=c_g[h][:].bitcast(I32).rearrange("p u n -> p n u"))
 
         def quant_c(h):
-            nc.vector.quantize_mx(out=c_codes[h][:].bitcast(FP8X4), scales=c_scales[h][:], in_=c_w[h][:].rearrange("p n u -> p (n u)").bitcast(BF16))
+            nc.vector.quantize_mx(out=c_codes[h].bitcast(FP8X4), scales=c_scales[h][:], in_=c_w[h][:].rearrange("p n u -> p (n u)").bitcast(BF16))
 
         acc = [[ps.tile([P, HALF], F32, name="acc%d%d" % (h, m)) for m in range(2)] for h in range(2)]
         logit = [[tile([P, HALF], F32, "logit%d%d" % (h, m)) for m in range(2)] for h in range(2)]
@@ -143,12 +139,12 @@ def tile_attend_prefer_topk_kernel(tc, qT, k_words, k_scales, cT, kb, offs, offs
         def mm_k(h, m, start):
             rows = slice(m * P, (m + 1) * P)
             nc.tensor.matmul_mx(out=acc[h][m][:], lhsT=q_codes[:, rows].bitcast(FP8X4), lhsT_scale=q_scales[:, rows],
-                                rhs=kw_g[h][:].bitcast(FP8X4), rhs_scale=ks_g[:, h * HALF : (h + 1) * HALF], start=start, stop=not start)
+                                rhs=kw_g[:, h * HALF : (h + 1) * HALF].bitcast(FP8X4), rhs_scale=ks_g[:, h * HALF : (h + 1) * HALF], start=start, stop=not start)
 
         def mm_c(h, m, start):
             rows = slice(NQ + m * P, NQ + (m + 1) * P)
             nc.tensor.matmul_mx(out=acc[h][m][:], lhsT=q_codes[:, rows].bitcast(FP8X4), lhsT_scale=q_scales[:, rows],
-                                rhs=c_codes[h][:].bitcast(FP8X4), rhs_scale=c_scales[h][:], start=start, stop=not start)
+                                rhs=c_codes[h].bitcast(FP8X4), rhs_scale=c_scales[h][:], start=start, stop=not start)
 
         def finish(h, m):
             cols = slice(h * HALF, (h + 1) * HALF)
@@ -156,42 +152,47 @@ def tile_attend_prefer_topk_kernel(tc, qT, k_words, k_scales, cT, kb, offs, offs
             nc.scalar.activation(out=prob[h][m][:], in_=logit[h][m][:], func=ACT.Sigmoid)
             nc.sync.dma_start(out=out[0, m * P : (m + 1) * P, cols], in_=prob[h][m][:])
 
-        load_ks(nc.gpsimd)
-        make_identity(nc, ident[:])
-        load_kb(nc.scalar)
-        load_lists()
+        load_ks(nc.sync)
+        nc.sync.dma_start(list1[:], offs)
         load_q()
         load_c(0, 0)
         load_c(0, 1)
+        load_kb(nc.sync)
+        nc.sync.dma_start(list2[:], offs2)
         load_c(1, 0)
         load_c(1, 1)
         load_kw()
+        make_identity(nc, ident[:])
+        gather_ks()
         cast_q()
         negate_q()
+        q_codes = tile([P, 2 * NQ], U32, "q_codes")
+        quant_q(q_codes)
+        c_g = [tile([P, 2, HALF], U32, "c_g0"), tile([P, 2, HALF], U32, "c_g1")]
         cast_c(0, 0)
         cast_c(0, 1)
-        gather_kb()
-        quant_q()
-        spread_kb()
-        cast_c(1, 0)
-        cast_c(1, 1)
         gather_c(0, 0)
         gather_c(0, 1)
-        gather_ks()
+        gather_kb()
+        cast_c(1, 0)
+        cast_c(1, 1)
+        turn_kb()
         gather_c(1, 0)
         weave(0)
         gather_c(1, 1)
         weave(1)
-        gather_kw(0)
-        quant_c(0)
-        for m in range(2):
-            mm_k(0, m, True)
-            mm_c(0, m, False)
-        gather_kw(1)
-        quant_c(1)
-        for m in range(2):
-            mm_k(1, m, True)
-            mm_c(1, m, False)
+        kb_all = tile([P, N], F32, "kb_all", tag="c_g1")
+        spread_kb()
+        gather_kw()
+        c_codes_all = tile([P, N], U32, "c_codes", tag="kw_win")
+        c_codes = [c_codes_all[:, h * HALF : (h + 1) * HALF] for h in range(2)]
+        for h in range(2):
+            for m in range(2):
+                mm_k(h, m, True)
+        for h in range(2):
+            quant_c(h)
+            for m in range(2):
+                mm_c(h, m, False)
         for h in range(2):
             for m in range(2):
                 finish(h, m)

@@ -152,9 +152,9 @@ def tile_attend_prefer_topk_kernel(tc, qT, k_words, k_scales, cT, kb, offs, offs
             nc.scalar.activation(out=prob[h][m][:], in_=logit[h][m][:], func=ACT.Sigmoid)
             nc.sync.dma_start(out=out[0, m * P : (m + 1) * P, cols], in_=prob[h][m][:])
 
-        load_ks(nc.sync)
-        nc.sync.dma_start(list1[:], offs)
         load_q()
+        nc.sync.dma_start(list1[:], offs)
+        load_ks(nc.sync)
         load_c(0, 0)
         load_c(0, 1)
         load_kb(nc.sync)

@@ -16,6 +16,10 @@ ALU = mybir.AluOpType
 P = 128
 D, NQ, N, T, T2 = 512, 256, 512, 2048, 1024
 HALF = N // 2
+CHUNK = T2 // 2
+KB_ROW = 16
+SCALAR_COLS = 192
+KB_SPLIT = 1152
 FLOPS = 2 * 2 * NQ * N * D
 BYTES = 4 * D * NQ + D * T + 16 * T + 4 * D * T2 + 4 * T + 2 * 2 * P * (N // 16) + 4 * NQ * N
 
@@ -35,23 +39,21 @@ def tile_attend_prefer_topk_kernel(tc, qT, k_words, k_scales, cT, kb, offs, offs
         ks_win = tile([P, T], U8, "ks_win")
         kw_win = tile([P, T], I32, "kw_win")
         q_raw = tile([P, 4, NQ], F32, "q_raw")
-        CH = [[(0, 512), (512, 1024)], [(0, 512), (512, 1024)]]
-        c_raw = [[tile([P, 2, b - a], F32, "c_raw%d_%d" % (u, a)) for a, b in CH[u]] for u in range(2)]
+        c_raw = [[tile([P, 2, CHUNK], F32, "c_raw%d_%d" % (u, i)) for i in range(2)] for u in range(2)]
         c_pair = [tile([P, T2, 2], BF16, "c_pair%d" % u) for u in range(2)]
         warm = tile([P, 2], F32, "warm")
         ident = tile([P, P], F32, "ident")
 
         nc.vector.memset(warm[:, 0:1], 0.0)
         nc.scalar.activation(out=warm[:, 1:2], in_=warm[:, 0:1], func=ACT.Sigmoid)
-        nc.vector.memset(kb_win[:, 0:1024].bitcast(I32), 0)
         nc.gpsimd.memset(ks_win[:].bitcast(I32), 0)
-        nc.gpsimd.memset(kb_win[:, 1024:T].bitcast(I32), 0)
+        nc.vector.memset(kb_win[:, 0:KB_SPLIT].bitcast(I32), 0)
+        nc.gpsimd.memset(kb_win[:, KB_SPLIT:T].bitcast(I32), 0)
 
         c_rows = cT.rearrange("(p t) n -> p t n", t=4)
 
         def load_c(u, i):
-            a, b = CH[u][i]
-            nc.sync.dma_start(out=c_raw[u][i][:], in_=c_rows[:, 2 * u : 2 * u + 2, a:b])
+            nc.sync.dma_start(out=c_raw[u][i][:], in_=c_rows[:, 2 * u : 2 * u + 2, i * CHUNK : (i + 1) * CHUNK])
 
         def load_q():
             nc.sync.dma_start(out=q_raw[:], in_=qT[0].rearrange("(p t) n -> p t n", t=4))
@@ -60,34 +62,29 @@ def tile_attend_prefer_topk_kernel(tc, qT, k_words, k_scales, cT, kb, offs, offs
             nc.sync.dma_start(out=kw_win[:], in_=k_words[0].rearrange("p n t -> p (n t)").bitcast(I32))
 
         def load_kb(eng):
-            eng.dma_start(out=kb_win[0:1, :], in_=kb[0:1, :])
+            eng.dma_start(out=kb_win[KB_ROW : KB_ROW + 1, :], in_=kb[0:1, :])
 
         def load_ks(eng):
             for r in range(4):
                 eng.dma_start(out=ks_win[r:P:32, :].bitcast(I32), in_=k_scales[0, r:16:4, :].bitcast(I32))
 
-
-        q_bf = tile([P, 2, NQ, 4], BF16, "q_bf")
-        q_scales = tile([P, 2 * NQ], U8, "q_scales")
+        q_bf = tile([P, NQ, 4], BF16, "q_bf")
+        q_codes = tile([P, NQ], U32, "q_codes")
+        q_scales = tile([P, NQ], U8, "q_scales")
 
         def cast_q():
-            nc.scalar.copy(out=q_bf[:, 0], in_=q_raw[:].rearrange("p t n -> p n t"))
+            nc.scalar.copy(out=q_bf[:], in_=q_raw[:].rearrange("p t n -> p n t"))
 
-        def negate_q():
-            nc.vector.tensor_scalar(out=q_bf[:, 1], in0=q_raw[:].rearrange("p t n -> p n t"), scalar1=-1.0, scalar2=None, op0=ALU.mult)
+        def quant_q():
+            nc.vector.quantize_mx(out=q_codes[:].bitcast(FP8X4), scales=q_scales[:], in_=q_bf[:].rearrange("p n t -> p (n t)"))
 
-        def quant_q(q_codes):
-            nc.vector.quantize_mx(out=q_codes[:].bitcast(FP8X4), scales=q_scales[:], in_=q_bf[:].rearrange("p s n t -> p (s n t)"))
-
-        def cast_c(u, i, eng="s", lo=None, hi=None):
-            a, b = CH[u][i]
-            lo = a if lo is None else lo
-            hi = b if hi is None else hi
-            src = c_raw[u][i][:, :, lo - a : hi - a].rearrange("p t n -> p n t")
+        def cast_c(u, i, eng="s", lo=0, hi=CHUNK):
+            src = c_raw[u][i][:, :, lo:hi].rearrange("p t n -> p n t")
+            dst = c_pair[u][:, i * CHUNK + lo : i * CHUNK + hi, :]
             if eng == "s":
-                nc.scalar.activation(out=c_pair[u][:, lo:hi, :], in_=src, func=ACT.Copy)
+                nc.scalar.activation(out=dst, in_=src, func=ACT.Copy)
             else:
-                nc.vector.tensor_copy(out=c_pair[u][:, lo:hi, :], in_=src)
+                nc.vector.tensor_copy(out=dst, in_=src)
 
         kb_g = tile([P, N], F32, "kb_g")
         turn1 = ps.tile([P, N], F32, name="turn1")
@@ -97,54 +94,50 @@ def tile_attend_prefer_topk_kernel(tc, qT, k_words, k_scales, cT, kb, offs, offs
             nc.vector.tensor_copy(out=kb_g[:], in_=kb_win[:].indirect(list1[:]))
 
         def turn_kb():
-            kb_col = tile([P, 4], F32, "kb_col", tag="c_raw1_512")
+            kb_col = tile([P, 4], F32, "kb_col", tag="c_raw1_1")
             for j in range(4):
                 nc.tensor.transpose(turn1[:, j * P : (j + 1) * P], kb_g[:, j * P : (j + 1) * P], ident[:])
-            nc.scalar.copy(out=kb_col[:], in_=turn1[:, 0:N:P])
+            nc.scalar.copy(out=kb_col[:], in_=turn1[:, KB_ROW:N:P])
             for j in range(4):
                 nc.tensor.transpose(turn2[:, j * P : (j + 1) * P], kb_col[:, j : j + 1].to_broadcast([P, P]), ident[:])
 
-        def spread_kb():
-            nc.scalar.copy(out=kb_all[:], in_=turn2[:])
-
         ks_g = tile([P, N], U8, "ks_g")
-        kw_g = tile([P, N], U32, "kw_g")
-        c_w = [tile([P, HALF, 2], U32, "c_w%d" % h) for h in range(2)]
+        kw_g = [tile([P, HALF], U32, "kw_g%d" % h) for h in range(2)]
+        c_g = [tile([P, 2, HALF], U32, "c_g%d" % h) for h in range(2)]
+        c_w = [tile([P, HALF, 2, 2], BF16, "c_w%d" % h) for h in range(2)]
         c_scales = [tile([P, HALF], U8, "c_scales%d" % h) for h in range(2)]
         W = HALF // 16
 
         def gather_ks():
             nc.vector.tensor_copy(out=ks_g[:], in_=ks_win[:].indirect(list1[:]))
 
-        def gather_kw():
-            nc.vector.tensor_copy(out=kw_g[:], in_=kw_win[:].bitcast(U32).indirect(list1[:]))
+        def gather_kw(h):
+            nc.vector.tensor_copy(out=kw_g[h][:], in_=kw_win[:].bitcast(U32).indirect(list1[:, h * W : (h + 1) * W]))
 
         def gather_c(u, h):
             win = c_pair[u][:].rearrange("p n t -> p (n t)").bitcast(U32)
             nc.vector.tensor_copy(out=c_g[h][:, u, :], in_=win.indirect(list2[:, h * W : (h + 1) * W]))
 
-        def weave(h, eng="s"):
-            if eng == "s":
-                nc.scalar.copy(out=c_w[h][:], in_=c_g[h][:].rearrange("p u n -> p n u"))
-            else:
-                nc.vector.tensor_copy(out=c_w[h][:].rearrange("p n u -> p (n u)").bitcast(I32).rearrange("p (n u) -> p n u", u=2), in_=c_g[h][:].bitcast(I32).rearrange("p u n -> p n u"))
+        def weave(h):
+            src = c_g[h][:].rearrange("p u n -> p (u n)").bitcast(BF16).rearrange("p (u n e) -> p n u e", u=2, e=2)
+            nc.vector.tensor_scalar(out=c_w[h][:], in0=src, scalar1=-1.0, scalar2=None, op0=ALU.mult)
 
         def quant_c(h):
-            nc.vector.quantize_mx(out=c_codes[h].bitcast(FP8X4), scales=c_scales[h][:], in_=c_w[h][:].rearrange("p n u -> p (n u)").bitcast(BF16))
+            nc.vector.quantize_mx(out=c_codes[h].bitcast(FP8X4), scales=c_scales[h][:], in_=c_w[h][:].rearrange("p n u e -> p (n u e)"))
 
         acc = [[ps.tile([P, HALF], F32, name="acc%d%d" % (h, m)) for m in range(2)] for h in range(2)]
         logit = [[tile([P, HALF], F32, "logit%d%d" % (h, m)) for m in range(2)] for h in range(2)]
         prob = [[tile([P, HALF], F32, "prob%d%d" % (h, m)) for m in range(2)] for h in range(2)]
 
-        def mm_k(h, m, start):
+        def mm_c(h, m):
             rows = slice(m * P, (m + 1) * P)
             nc.tensor.matmul_mx(out=acc[h][m][:], lhsT=q_codes[:, rows].bitcast(FP8X4), lhsT_scale=q_scales[:, rows],
-                                rhs=kw_g[:, h * HALF : (h + 1) * HALF].bitcast(FP8X4), rhs_scale=ks_g[:, h * HALF : (h + 1) * HALF], start=start, stop=not start)
+                                rhs=c_codes[h].bitcast(FP8X4), rhs_scale=c_scales[h][:], start=True, stop=False)
 
-        def mm_c(h, m, start):
-            rows = slice(NQ + m * P, NQ + (m + 1) * P)
+        def mm_k(h, m):
+            rows = slice(m * P, (m + 1) * P)
             nc.tensor.matmul_mx(out=acc[h][m][:], lhsT=q_codes[:, rows].bitcast(FP8X4), lhsT_scale=q_scales[:, rows],
-                                rhs=c_codes[h].bitcast(FP8X4), rhs_scale=c_scales[h][:], start=start, stop=not start)
+                                rhs=kw_g[h][:].bitcast(FP8X4), rhs_scale=ks_g[:, h * HALF : (h + 1) * HALF], start=False, stop=True)
 
         def finish(h, m):
             cols = slice(h * HALF, (h + 1) * HALF)
@@ -152,47 +145,46 @@ def tile_attend_prefer_topk_kernel(tc, qT, k_words, k_scales, cT, kb, offs, offs
             nc.scalar.activation(out=prob[h][m][:], in_=logit[h][m][:], func=ACT.Sigmoid)
             nc.sync.dma_start(out=out[0, m * P : (m + 1) * P, cols], in_=prob[h][m][:])
 
-        load_q()
         nc.sync.dma_start(list1[:], offs)
         load_ks(nc.sync)
         load_c(0, 0)
-        load_c(0, 1)
         load_kb(nc.sync)
+        load_c(0, 1)
         nc.sync.dma_start(list2[:], offs2)
         load_c(1, 0)
         load_c(1, 1)
+        load_q()
         load_kw()
         make_identity(nc, ident[:])
         gather_ks()
-        cast_q()
-        negate_q()
-        q_codes = tile([P, 2 * NQ], U32, "q_codes")
-        quant_q(q_codes)
-        c_g = [tile([P, 2, HALF], U32, "c_g0"), tile([P, 2, HALF], U32, "c_g1")]
         cast_c(0, 0)
-        cast_c(0, 1)
+        gather_kb()
+        cast_c(0, 1, "s", 0, SCALAR_COLS)
+        cast_c(0, 1, "v", SCALAR_COLS, CHUNK)
         gather_c(0, 0)
         gather_c(0, 1)
-        gather_kb()
         cast_c(1, 0)
-        cast_c(1, 1)
+        cast_c(1, 1, "s", 0, SCALAR_COLS)
+        cast_c(1, 1, "v", SCALAR_COLS, CHUNK)
         turn_kb()
         gather_c(1, 0)
-        weave(0)
         gather_c(1, 1)
+        cast_q()
+        weave(0)
         weave(1)
-        kb_all = tile([P, N], F32, "kb_all", tag="c_g1")
-        spread_kb()
-        gather_kw()
-        c_codes_all = tile([P, N], U32, "c_codes", tag="kw_win")
+        quant_q()
+        kb_all = tile([P, N], F32, "kb_all", tag="q_raw")
+        nc.scalar.copy(out=kb_all[:], in_=turn2[:])
+        c_codes_all = tile([P, N], U32, "c_codes", tag="q_bf")
         c_codes = [c_codes_all[:, h * HALF : (h + 1) * HALF] for h in range(2)]
-        for h in range(2):
-            for m in range(2):
-                mm_k(h, m, True)
         for h in range(2):
             quant_c(h)
             for m in range(2):
-                mm_c(h, m, False)
+                mm_c(h, m)
+        for h in range(2):
+            gather_kw(h)
+            for m in range(2):
+                mm_k(h, m)
         for h in range(2):
             for m in range(2):
                 finish(h, m)

@@ -17,9 +17,10 @@ P = 128
 D, NQ, N, T, T2 = 512, 256, 512, 2048, 1024
 HALF = N // 2
 CHUNK = T2 // 2
-KB_ROW = 16
+KB_ROW = 127
 SCALAR_COLS = 192
 KB_SPLIT = 1152
+KS_ROW = P - 16
 FLOPS = 2 * 2 * NQ * N * D
 BYTES = 4 * D * NQ + D * T + 16 * T + 4 * D * T2 + 4 * T + 2 * 2 * P * (N // 16) + 4 * NQ * N
 
@@ -46,9 +47,9 @@ def tile_attend_prefer_topk_kernel(tc, qT, k_words, k_scales, cT, kb, offs, offs
 
         nc.vector.memset(warm[:, 0:1], 0.0)
         nc.scalar.activation(out=warm[:, 1:2], in_=warm[:, 0:1], func=ACT.Sigmoid)
-        nc.gpsimd.memset(ks_win[:].bitcast(I32), 0)
-        nc.vector.memset(kb_win[:, 0:KB_SPLIT].bitcast(I32), 0)
-        nc.gpsimd.memset(kb_win[:, KB_SPLIT:T].bitcast(I32), 0)
+        nc.gpsimd.memset(ks_win[0:KS_ROW, :].bitcast(I32), 0)
+        nc.vector.memset(kb_win[0:KB_ROW, 0:KB_SPLIT].bitcast(I32), 0)
+        nc.gpsimd.memset(kb_win[0:KB_ROW, KB_SPLIT:T].bitcast(I32), 0)
 
         c_rows = cT.rearrange("(p t) n -> p t n", t=4)
 
@@ -65,8 +66,7 @@ def tile_attend_prefer_topk_kernel(tc, qT, k_words, k_scales, cT, kb, offs, offs
             eng.dma_start(out=kb_win[KB_ROW : KB_ROW + 1, :], in_=kb[0:1, :])
 
         def load_ks(eng):
-            for r in range(4):
-                eng.dma_start(out=ks_win[r:P:32, :].bitcast(I32), in_=k_scales[0, r:16:4, :].bitcast(I32))
+            eng.dma_start(out=ks_win[KS_ROW:P, :].bitcast(I32), in_=k_scales[0].bitcast(I32))
 
         q_bf = tile([P, NQ, 4], BF16, "q_bf")
         q_codes = tile([P, NQ], U32, "q_codes")
@@ -102,6 +102,7 @@ def tile_attend_prefer_topk_kernel(tc, qT, k_words, k_scales, cT, kb, offs, offs
                 nc.tensor.transpose(turn2[:, j * P : (j + 1) * P], kb_col[:, j : j + 1].to_broadcast([P, P]), ident[:])
 
         ks_g = tile([P, N], U8, "ks_g")
+        k_plane = tile([P, N], U8, "k_plane")
         kw_g = [tile([P, HALF], U32, "kw_g%d" % h) for h in range(2)]
         c_g = [tile([P, 2, HALF], U32, "c_g%d" % h) for h in range(2)]
         c_w = [tile([P, HALF, 2, 2], BF16, "c_w%d" % h) for h in range(2)]
@@ -110,6 +111,10 @@ def tile_attend_prefer_topk_kernel(tc, qT, k_words, k_scales, cT, kb, offs, offs
 
         def gather_ks():
             nc.vector.tensor_copy(out=ks_g[:], in_=ks_win[:].indirect(list1[:]))
+
+        def place_ks(eng):
+            for quad in range(4):
+                eng.dma_start(out=k_plane[32 * quad : 32 * quad + 4, :].bitcast(I32), in_=ks_g[KS_ROW + 4 * quad : KS_ROW + 4 * quad + 4, :].bitcast(I32))
 
         def gather_kw(h):
             nc.vector.tensor_copy(out=kw_g[h][:], in_=kw_win[:].bitcast(U32).indirect(list1[:, h * W : (h + 1) * W]))
@@ -137,7 +142,7 @@ def tile_attend_prefer_topk_kernel(tc, qT, k_words, k_scales, cT, kb, offs, offs
         def mm_k(h, m):
             rows = slice(m * P, (m + 1) * P)
             nc.tensor.matmul_mx(out=acc[h][m][:], lhsT=q_codes[:, rows].bitcast(FP8X4), lhsT_scale=q_scales[:, rows],
-                                rhs=kw_g[h][:].bitcast(FP8X4), rhs_scale=ks_g[:, h * HALF : (h + 1) * HALF], start=False, stop=True)
+                                rhs=kw_g[h][:].bitcast(FP8X4), rhs_scale=k_plane[:, h * HALF : (h + 1) * HALF], start=False, stop=True)
 
         def finish(h, m):
             cols = slice(h * HALF, (h + 1) * HALF)
@@ -147,8 +152,8 @@ def tile_attend_prefer_topk_kernel(tc, qT, k_words, k_scales, cT, kb, offs, offs
 
         nc.sync.dma_start(list1[:], offs)
         load_ks(nc.sync)
-        load_c(0, 0)
         load_kb(nc.sync)
+        load_c(0, 0)
         load_c(0, 1)
         nc.sync.dma_start(list2[:], offs2)
         load_c(1, 0)
@@ -157,6 +162,7 @@ def tile_attend_prefer_topk_kernel(tc, qT, k_words, k_scales, cT, kb, offs, offs
         load_kw()
         make_identity(nc, ident[:])
         gather_ks()
+        place_ks(nc.gpsimd)
         cast_c(0, 0)
         gather_kb()
         cast_c(0, 1, "s", 0, SCALAR_COLS)

@@ -21,6 +21,7 @@ KB_ROW = 127
 SCALAR_COLS = 192
 KB_SPLIT = 1152
 KS_ROW = P - 16
+PIECES = [(0, 0, 128), (0, 128, 256), (1, 0, 256), (0, 256, 512), (1, 256, 384), (1, 384, 512)]
 FLOPS = 2 * 2 * NQ * N * D
 BYTES = 4 * D * NQ + D * T + 16 * T + 4 * D * T2 + 4 * T + 2 * 2 * P * (N // 16) + 4 * NQ * N
 
@@ -75,8 +76,9 @@ def tile_attend_prefer_topk_kernel(tc, qT, k_words, k_scales, cT, kb, offs, offs
         def cast_q():
             nc.scalar.copy(out=q_bf[:], in_=q_raw[:].rearrange("p t n -> p n t"))
 
-        def quant_q():
-            nc.vector.quantize_mx(out=q_codes[:].bitcast(FP8X4), scales=q_scales[:], in_=q_bf[:].rearrange("p n t -> p (n t)"))
+        def quant_q(m):
+            rows = slice(m * P, (m + 1) * P)
+            nc.vector.quantize_mx(out=q_codes[:, rows].bitcast(FP8X4), scales=q_scales[:, rows], in_=q_bf[:, rows, :].rearrange("p n t -> p (n t)"))
 
         def cast_c(u, i, eng="s", lo=0, hi=CHUNK):
             src = c_raw[u][i][:, :, lo:hi].rearrange("p t n -> p n t")
@@ -103,10 +105,10 @@ def tile_attend_prefer_topk_kernel(tc, qT, k_words, k_scales, cT, kb, offs, offs
 
         ks_g = tile([P, N], U8, "ks_g")
         k_plane = tile([P, N], U8, "k_plane")
-        kw_g = [tile([P, HALF], U32, "kw_g%d" % h) for h in range(2)]
+        kw_g = tile([P, N], U32, "kw_g")
         c_g = [tile([P, 2, HALF], U32, "c_g%d" % h) for h in range(2)]
         c_w = [tile([P, HALF, 2, 2], BF16, "c_w%d" % h) for h in range(2)]
-        c_scales = [tile([P, HALF], U8, "c_scales%d" % h) for h in range(2)]
+        c_scales = tile([P, N], U8, "c_scales")
         W = HALF // 16
 
         def gather_ks():
@@ -117,7 +119,7 @@ def tile_attend_prefer_topk_kernel(tc, qT, k_words, k_scales, cT, kb, offs, offs
                 eng.dma_start(out=k_plane[32 * quad : 32 * quad + 4, :].bitcast(I32), in_=ks_g[KS_ROW + 4 * quad : KS_ROW + 4 * quad + 4, :].bitcast(I32))
 
         def gather_kw(h):
-            nc.vector.tensor_copy(out=kw_g[h][:], in_=kw_win[:].bitcast(U32).indirect(list1[:, h * W : (h + 1) * W]))
+            nc.vector.tensor_copy(out=kw_g[:, h * HALF : (h + 1) * HALF], in_=kw_win[:].bitcast(U32).indirect(list1[:, h * W : (h + 1) * W]))
 
         def gather_c(u, h):
             win = c_pair[u][:].rearrange("p n t -> p (n t)").bitcast(U32)
@@ -128,27 +130,29 @@ def tile_attend_prefer_topk_kernel(tc, qT, k_words, k_scales, cT, kb, offs, offs
             nc.vector.tensor_scalar(out=c_w[h][:], in0=src, scalar1=-1.0, scalar2=None, op0=ALU.mult)
 
         def quant_c(h):
-            nc.vector.quantize_mx(out=c_codes[h].bitcast(FP8X4), scales=c_scales[h][:], in_=c_w[h][:].rearrange("p n u e -> p (n u e)"))
+            nc.vector.quantize_mx(out=c_codes[:, h * HALF : (h + 1) * HALF].bitcast(FP8X4), scales=c_scales[:, h * HALF : (h + 1) * HALF], in_=c_w[h][:].rearrange("p n u e -> p (n u e)"))
 
-        acc = [[ps.tile([P, HALF], F32, name="acc%d%d" % (h, m)) for m in range(2)] for h in range(2)]
-        logit = [[tile([P, HALF], F32, "logit%d%d" % (h, m)) for m in range(2)] for h in range(2)]
-        prob = [[tile([P, HALF], F32, "prob%d%d" % (h, m)) for m in range(2)] for h in range(2)]
+        acc = [ps.tile([P, b - a], F32, name="acc%d" % i) for i, (m, a, b) in enumerate(PIECES)]
+        logit = [tile([P, b - a], F32, "logit%d" % i) for i, (m, a, b) in enumerate(PIECES)]
+        prob = [tile([P, b - a], F32, "prob%d" % i) for i, (m, a, b) in enumerate(PIECES)]
 
-        def mm_c(h, m):
+        def mm_c(i, start):
+            m, a, b = PIECES[i]
             rows = slice(m * P, (m + 1) * P)
-            nc.tensor.matmul_mx(out=acc[h][m][:], lhsT=q_codes[:, rows].bitcast(FP8X4), lhsT_scale=q_scales[:, rows],
-                                rhs=c_codes[h].bitcast(FP8X4), rhs_scale=c_scales[h][:], start=True, stop=False)
+            nc.tensor.matmul_mx(out=acc[i][:], lhsT=q_codes[:, rows].bitcast(FP8X4), lhsT_scale=q_scales[:, rows],
+                                rhs=c_codes[:, a:b].bitcast(FP8X4), rhs_scale=c_scales[:, a:b], start=start, stop=not start)
 
-        def mm_k(h, m):
+        def mm_k(i, start):
+            m, a, b = PIECES[i]
             rows = slice(m * P, (m + 1) * P)
-            nc.tensor.matmul_mx(out=acc[h][m][:], lhsT=q_codes[:, rows].bitcast(FP8X4), lhsT_scale=q_scales[:, rows],
-                                rhs=kw_g[h][:].bitcast(FP8X4), rhs_scale=k_plane[:, h * HALF : (h + 1) * HALF], start=False, stop=True)
+            nc.tensor.matmul_mx(out=acc[i][:], lhsT=q_codes[:, rows].bitcast(FP8X4), lhsT_scale=q_scales[:, rows],
+                                rhs=kw_g[:, a:b].bitcast(FP8X4), rhs_scale=k_plane[:, a:b], start=start, stop=not start)
 
-        def finish(h, m):
-            cols = slice(h * HALF, (h + 1) * HALF)
-            nc.vector.tensor_tensor(out=logit[h][m][:], in0=acc[h][m][:], in1=kb_all[:, cols], op=ALU.add)
-            nc.scalar.activation(out=prob[h][m][:], in_=logit[h][m][:], func=ACT.Sigmoid)
-            nc.sync.dma_start(out=out[0, m * P : (m + 1) * P, cols], in_=prob[h][m][:])
+        def finish(i, eng):
+            m, a, b = PIECES[i]
+            nc.vector.tensor_tensor(out=logit[i][:], in0=acc[i][:], in1=kb_all[:, a:b], op=ALU.add)
+            nc.scalar.activation(out=prob[i][:], in_=logit[i][:], func=ACT.Sigmoid)
+            eng.dma_start(out=out[0, m * P : (m + 1) * P, a:b], in_=prob[i][:])
 
         nc.sync.dma_start(list1[:], offs)
         load_ks(nc.sync)
@@ -162,7 +166,7 @@ def tile_attend_prefer_topk_kernel(tc, qT, k_words, k_scales, cT, kb, offs, offs
         load_kw()
         make_identity(nc, ident[:])
         gather_ks()
-        place_ks(nc.gpsimd)
+        place_ks(nc.sync)
         cast_c(0, 0)
         gather_kb()
         cast_c(0, 1, "s", 0, SCALAR_COLS)
@@ -178,19 +182,18 @@ def tile_attend_prefer_topk_kernel(tc, qT, k_words, k_scales, cT, kb, offs, offs
         cast_q()
         weave(0)
         weave(1)
-        quant_q()
-        kb_all = tile([P, N], F32, "kb_all", tag="q_raw")
+        quant_q(0)
+        c_codes = tile([P, N], U32, "c_codes", tag="q_raw")
+        quant_c(0)
+        quant_q(1)
+        kb_all = tile([P, N], F32, "kb_all", tag="q_bf")
         nc.scalar.copy(out=kb_all[:], in_=turn2[:])
-        c_codes_all = tile([P, N], U32, "c_codes", tag="q_bf")
-        c_codes = [c_codes_all[:, h * HALF : (h + 1) * HALF] for h in range(2)]
-        for h in range(2):
-            quant_c(h)
-            for m in range(2):
-                mm_c(h, m)
-        for h in range(2):
-            gather_kw(h)
-            for m in range(2):
-                mm_k(h, m)
-        for h in range(2):
-            for m in range(2):
-                finish(h, m)
+        quant_c(1)
+        for i in range(len(PIECES)):
+            mm_c(i, True)
+        gather_kw(0)
+        gather_kw(1)
+        for i in range(len(PIECES)):
+            mm_k(i, False)
+        for i in range(len(PIECES)):
+            finish(i, nc.sync)

@@ -16,12 +16,11 @@ ALU = mybir.AluOpType
 P = 128
 D, NQ, N, T, T2 = 512, 256, 512, 2048, 1024
 HALF = N // 2
-CHUNK = T2 // 2
+CHUNKS = [(0, 0, 512, 512), (0, 512, 1024, 192), (1, 0, 512, 512), (1, 512, 1024, 192)]
 KB_ROW = 127
-SCALAR_COLS = 192
 KB_SPLIT = 1152
 KS_ROW = P - 16
-PIECES = [(0, 0, 128), (0, 128, 256), (1, 0, 256), (0, 256, 512), (1, 256, 384), (1, 384, 512)]
+PIECES = [(0, 0, 128), (0, 128, 256), (1, 0, 256), (0, 256, 384), (1, 256, 384), (0, 384, 512), (1, 384, 512)]
 FLOPS = 2 * 2 * NQ * N * D
 BYTES = 4 * D * NQ + D * T + 16 * T + 4 * D * T2 + 4 * T + 2 * 2 * P * (N // 16) + 4 * NQ * N
 
@@ -41,7 +40,7 @@ def tile_attend_prefer_topk_kernel(tc, qT, k_words, k_scales, cT, kb, offs, offs
         ks_win = tile([P, T], U8, "ks_win")
         kw_win = tile([P, T], I32, "kw_win")
         q_raw = tile([P, 4, NQ], F32, "q_raw")
-        c_raw = [[tile([P, 2, CHUNK], F32, "c_raw%d_%d" % (u, i)) for i in range(2)] for u in range(2)]
+        c_raw = [tile([P, 2, b - a], F32, "c_raw%d" % i) for i, (u, a, b, s) in enumerate(CHUNKS)]
         c_pair = [tile([P, T2, 2], BF16, "c_pair%d" % u) for u in range(2)]
         warm = tile([P, 2], F32, "warm")
         ident = tile([P, P], F32, "ident")
@@ -54,8 +53,9 @@ def tile_attend_prefer_topk_kernel(tc, qT, k_words, k_scales, cT, kb, offs, offs
 
         c_rows = cT.rearrange("(p t) n -> p t n", t=4)
 
-        def load_c(u, i):
-            nc.sync.dma_start(out=c_raw[u][i][:], in_=c_rows[:, 2 * u : 2 * u + 2, i * CHUNK : (i + 1) * CHUNK])
+        def load_c(i):
+            u, a, b, s = CHUNKS[i]
+            nc.sync.dma_start(out=c_raw[i][:], in_=c_rows[:, 2 * u : 2 * u + 2, a:b])
 
         def load_q():
             nc.sync.dma_start(out=q_raw[:], in_=qT[0].rearrange("(p t) n -> p t n", t=4))
@@ -74,29 +74,27 @@ def tile_attend_prefer_topk_kernel(tc, qT, k_words, k_scales, cT, kb, offs, offs
         q_scales = tile([P, NQ], U8, "q_scales")
 
         def cast_q():
-            nc.scalar.copy(out=q_bf[:], in_=q_raw[:].rearrange("p t n -> p n t"))
+            nc.scalar.copy(out=q_bf[:].rearrange("p (c i) t -> p c t i", i=4), in_=q_raw[:].rearrange("p t (c i) -> p c t i", i=4))
 
-        def quant_q(m):
-            rows = slice(m * P, (m + 1) * P)
-            nc.vector.quantize_mx(out=q_codes[:, rows].bitcast(FP8X4), scales=q_scales[:, rows], in_=q_bf[:, rows, :].rearrange("p n t -> p (n t)"))
+        def quant_q():
+            nc.vector.quantize_mx(out=q_codes[:].bitcast(FP8X4), scales=q_scales[:], in_=q_bf[:].rearrange("p n t -> p (n t)"))
 
-        def cast_c(u, i, eng="s", lo=0, hi=CHUNK):
-            src = c_raw[u][i][:, :, lo:hi].rearrange("p t n -> p n t")
-            dst = c_pair[u][:, i * CHUNK + lo : i * CHUNK + hi, :]
-            if eng == "s":
-                nc.scalar.activation(out=dst, in_=src, func=ACT.Copy)
-            else:
-                nc.vector.tensor_copy(out=dst, in_=src)
+        def cast_c(i):
+            u, a, b, s = CHUNKS[i]
+            src = c_raw[i][:].rearrange("p t n -> p n t")
+            nc.scalar.activation(out=c_pair[u][:, a : a + s, :], in_=src[:, 0:s, :], func=ACT.Copy)
+            if a + s < b:
+                nc.vector.tensor_copy(out=c_pair[u][:, a + s : b, :], in_=src[:, s : b - a, :])
 
         kb_g = tile([P, N], F32, "kb_g")
-        turn1 = ps.tile([P, N], F32, name="turn1")
+        turn1 = ps.tile([P, N], F32, name="turn1", tag="turn1")
         turn2 = ps.tile([P, N], F32, name="turn2")
 
         def gather_kb():
             nc.vector.tensor_copy(out=kb_g[:], in_=kb_win[:].indirect(list1[:]))
 
         def turn_kb():
-            kb_col = tile([P, 4], F32, "kb_col", tag="c_raw1_1")
+            kb_col = tile([P, 4], F32, "kb_col", tag="c_raw%d" % (len(CHUNKS) - 1))
             for j in range(4):
                 nc.tensor.transpose(turn1[:, j * P : (j + 1) * P], kb_g[:, j * P : (j + 1) * P], ident[:])
             nc.scalar.copy(out=kb_col[:], in_=turn1[:, KB_ROW:N:P])
@@ -129,10 +127,12 @@ def tile_attend_prefer_topk_kernel(tc, qT, k_words, k_scales, cT, kb, offs, offs
             src = c_g[h][:].rearrange("p u n -> p (u n)").bitcast(BF16).rearrange("p (u n e) -> p n u e", u=2, e=2)
             nc.vector.tensor_scalar(out=c_w[h][:], in0=src, scalar1=-1.0, scalar2=None, op0=ALU.mult)
 
-        def quant_c(h):
-            nc.vector.quantize_mx(out=c_codes[:, h * HALF : (h + 1) * HALF].bitcast(FP8X4), scales=c_scales[:, h * HALF : (h + 1) * HALF], in_=c_w[h][:].rearrange("p n u e -> p (n u e)"))
+        def quant_c(codes, a, b):
+            h = a // HALF
+            nc.vector.quantize_mx(out=codes[:, a - h * HALF : b - h * HALF].bitcast(FP8X4), scales=c_scales[:, a:b],
+                                  in_=c_w[h][:, a - h * HALF : b - h * HALF].rearrange("p n u e -> p (n u e)"))
 
-        acc = [ps.tile([P, b - a], F32, name="acc%d" % i) for i, (m, a, b) in enumerate(PIECES)]
+        acc = [ps.tile([P, b - a], F32, name="acc%d" % i, tag="turn1" if i == 6 else "acc%d" % i) for i, (m, a, b) in enumerate(PIECES)]
         logit = [tile([P, b - a], F32, "logit%d" % i) for i, (m, a, b) in enumerate(PIECES)]
         prob = [tile([P, b - a], F32, "prob%d" % i) for i, (m, a, b) in enumerate(PIECES)]
 
@@ -140,7 +140,7 @@ def tile_attend_prefer_topk_kernel(tc, qT, k_words, k_scales, cT, kb, offs, offs
             m, a, b = PIECES[i]
             rows = slice(m * P, (m + 1) * P)
             nc.tensor.matmul_mx(out=acc[i][:], lhsT=q_codes[:, rows].bitcast(FP8X4), lhsT_scale=q_scales[:, rows],
-                                rhs=c_codes[:, a:b].bitcast(FP8X4), rhs_scale=c_scales[:, a:b], start=start, stop=not start)
+                                rhs=c_codes[a // HALF][:, a % HALF : a % HALF + b - a].bitcast(FP8X4), rhs_scale=c_scales[:, a:b], start=start, stop=not start)
 
         def mm_k(i, start):
             m, a, b = PIECES[i]
@@ -157,43 +157,46 @@ def tile_attend_prefer_topk_kernel(tc, qT, k_words, k_scales, cT, kb, offs, offs
         nc.sync.dma_start(list1[:], offs)
         load_ks(nc.sync)
         load_kb(nc.sync)
-        load_c(0, 0)
-        load_c(0, 1)
+        load_c(0)
+        load_c(1)
         nc.sync.dma_start(list2[:], offs2)
-        load_c(1, 0)
-        load_c(1, 1)
+        load_c(2)
+        load_c(3)
         load_q()
         load_kw()
         make_identity(nc, ident[:])
         gather_ks()
         place_ks(nc.sync)
-        cast_c(0, 0)
+        cast_c(0)
         gather_kb()
-        cast_c(0, 1, "s", 0, SCALAR_COLS)
-        cast_c(0, 1, "v", SCALAR_COLS, CHUNK)
+        cast_c(1)
         gather_c(0, 0)
         gather_c(0, 1)
-        cast_c(1, 0)
-        cast_c(1, 1, "s", 0, SCALAR_COLS)
-        cast_c(1, 1, "v", SCALAR_COLS, CHUNK)
+        cast_c(2)
+        cast_c(3)
         turn_kb()
         gather_c(1, 0)
         gather_c(1, 1)
         cast_q()
         weave(0)
         weave(1)
-        quant_q(0)
-        c_codes = tile([P, N], U32, "c_codes", tag="q_raw")
-        quant_c(0)
-        quant_q(1)
-        kb_all = tile([P, N], F32, "kb_all", tag="q_bf")
+        c_codes = [tile([P, HALF], U32, "c_codes0")]
+        quant_c(c_codes[0], 0, HALF)
+        quant_q()
+        kb_all = tile([P, N], F32, "kb_all", tag="q_raw")
         nc.scalar.copy(out=kb_all[:], in_=turn2[:])
-        quant_c(1)
-        for i in range(len(PIECES)):
+        for i in range(3):
             mm_c(i, True)
         gather_kw(0)
         gather_kw(1)
-        for i in range(len(PIECES)):
+        c_codes.append(tile([P, HALF], U32, "c_codes1", tag="kw_win"))
+        quant_c(c_codes[1], 256, 384)
+        quant_c(c_codes[1], 384, 512)
+        for i in range(3):
             mm_k(i, False)
+        for i in range(3, len(PIECES)):
+            mm_k(i, True)
+        for i in range(3, len(PIECES)):
+            mm_c(i, False)
         for i in range(len(PIECES)):
             finish(i, nc.sync)

@@ -16,7 +16,7 @@ ALU = mybir.AluOpType
 P = 128
 D, NQ, N, T, T2 = 512, 256, 512, 2048, 1024
 HALF = N // 2
-CHUNKS = [(0, 0, 512, 512), (0, 512, 1024, 192), (1, 0, 512, 512), (1, 512, 1024, 192)]
+CHUNKS = [(0, 0, 1024, 400), (1, 0, 1024, 384)]
 KB_ROW = 127
 KB_SPLIT = 1152
 KS_ROW = P - 16
@@ -29,6 +29,7 @@ def tile_attend_prefer_topk_kernel(tc, qT, k_words, k_scales, cT, kb, offs, offs
     nc = tc.nc
     with ExitStack() as ctx:
         sb = ctx.enter_context(tc.tile_pool(name="sb", bufs=1))
+        held = ctx.enter_context(tc.tile_pool(name="held", bufs=1))
         ps = ctx.enter_context(tc.psum_pool(name="ps", bufs=1))
 
         def tile(shape, dtype, name, tag=None):
@@ -39,7 +40,7 @@ def tile_attend_prefer_topk_kernel(tc, qT, k_words, k_scales, cT, kb, offs, offs
         kb_win = tile([P, T], F32, "kb_win")
         ks_win = tile([P, T], U8, "ks_win")
         kw_win = tile([P, T], I32, "kw_win")
-        q_raw = tile([P, 4, NQ], F32, "q_raw")
+        q_raw = held.tile([P, 4, NQ], F32, name="q_raw", align_bytes=64, offset=0)
         c_raw = [tile([P, 2, b - a], F32, "c_raw%d" % i) for i, (u, a, b, s) in enumerate(CHUNKS)]
         c_pair = [tile([P, T2, 2], BF16, "c_pair%d" % u) for u in range(2)]
         warm = tile([P, 2], F32, "warm")
@@ -105,7 +106,7 @@ def tile_attend_prefer_topk_kernel(tc, qT, k_words, k_scales, cT, kb, offs, offs
         k_plane = tile([P, N], U8, "k_plane")
         kw_g = tile([P, N], U32, "kw_g")
         c_g = [tile([P, 2, HALF], U32, "c_g%d" % h) for h in range(2)]
-        c_w = [tile([P, HALF, 2, 2], BF16, "c_w%d" % h) for h in range(2)]
+        c_w = [tile([P, HALF, 2, 2], BF16, "c_w0")]
         c_scales = tile([P, N], U8, "c_scales")
         W = HALF // 16
 
@@ -125,7 +126,11 @@ def tile_attend_prefer_topk_kernel(tc, qT, k_words, k_scales, cT, kb, offs, offs
 
         def weave(h):
             src = c_g[h][:].rearrange("p u n -> p (u n)").bitcast(BF16).rearrange("p (u n e) -> p n u e", u=2, e=2)
-            nc.vector.tensor_scalar(out=c_w[h][:], in0=src, scalar1=-1.0, scalar2=None, op0=ALU.mult)
+            if h == 0:
+                nc.vector.tensor_scalar(out=c_w[h][:], in0=src, scalar1=-1.0, scalar2=None, op0=ALU.mult)
+            else:
+                c_w.append(held.tile([P, HALF, 2, 2], BF16, name="c_w1", align_bytes=64, offset=0))
+                nc.scalar.activation(out=c_w[h][:], in_=src, func=ACT.Copy, scale=-1.0)
 
         def quant_c(codes, a, b):
             h = a // HALF
@@ -158,32 +163,28 @@ def tile_attend_prefer_topk_kernel(tc, qT, k_words, k_scales, cT, kb, offs, offs
         load_ks(nc.sync)
         load_kb(nc.sync)
         load_c(0)
-        load_c(1)
         nc.sync.dma_start(list2[:], offs2)
-        load_c(2)
-        load_c(3)
+        load_c(1)
         load_q()
         load_kw()
         make_identity(nc, ident[:])
         gather_ks()
         place_ks(nc.sync)
-        cast_c(0)
         gather_kb()
-        cast_c(1)
+        cast_c(0)
         gather_c(0, 0)
         gather_c(0, 1)
-        cast_c(2)
-        cast_c(3)
+        cast_c(1)
         turn_kb()
         gather_c(1, 0)
         gather_c(1, 1)
         cast_q()
         weave(0)
         weave(1)
-        c_codes = [tile([P, HALF], U32, "c_codes0")]
-        quant_c(c_codes[0], 0, HALF)
         quant_q()
-        kb_all = tile([P, N], F32, "kb_all", tag="q_raw")
+        c_codes = [held.tile([P, HALF], U32, name="c_codes0", align_bytes=64, offset=2048)]
+        quant_c(c_codes[0], 0, HALF)
+        kb_all = tile([P, N], F32, "kb_all", tag="q_bf")
         nc.scalar.copy(out=kb_all[:], in_=turn2[:])
         for i in range(3):
             mm_c(i, True)

@@ -16,11 +16,10 @@ ALU = mybir.AluOpType
 P = 128
 D, NQ, N, T, T2 = 512, 256, 512, 2048, 1024
 HALF = N // 2
-CHUNKS = [(0, 0, 1024, 400), (1, 0, 1024, 384)]
+CHUNKS = [(0, 0, 1024, 400), (1, 0, 1024, 400)]
 KB_ROW = 127
-KB_SPLIT = 1152
 KS_ROW = P - 16
-PIECES = [(0, 0, 128), (0, 128, 256), (1, 0, 256), (0, 256, 384), (1, 256, 384), (0, 384, 512), (1, 384, 512)]
+PIECES = [(0, 0, 256), (1, 0, 256), (0, 256, 384), (1, 256, 384), (0, 384, 512), (1, 384, 512)]
 FLOPS = 2 * 2 * NQ * N * D
 BYTES = 4 * D * NQ + D * T + 16 * T + 4 * D * T2 + 4 * T + 2 * 2 * P * (N // 16) + 4 * NQ * N
 
@@ -39,7 +38,6 @@ def tile_attend_prefer_topk_kernel(tc, qT, k_words, k_scales, cT, kb, offs, offs
         list2 = tile([P, N // 16], U16, "list2")
         kb_win = tile([P, T], F32, "kb_win")
         ks_win = tile([P, T], U8, "ks_win")
-        kw_win = tile([P, T], I32, "kw_win")
         q_raw = held.tile([P, 4, NQ], F32, name="q_raw", align_bytes=64, offset=0)
         c_raw = [tile([P, 2, b - a], F32, "c_raw%d" % i) for i, (u, a, b, s) in enumerate(CHUNKS)]
         c_pair = [tile([P, T2, 2], BF16, "c_pair%d" % u) for u in range(2)]
@@ -49,8 +47,7 @@ def tile_attend_prefer_topk_kernel(tc, qT, k_words, k_scales, cT, kb, offs, offs
         nc.vector.memset(warm[:, 0:1], 0.0)
         nc.scalar.activation(out=warm[:, 1:2], in_=warm[:, 0:1], func=ACT.Sigmoid)
         nc.gpsimd.memset(ks_win[0:KS_ROW, :].bitcast(I32), 0)
-        nc.vector.memset(kb_win[0:KB_ROW, 0:KB_SPLIT].bitcast(I32), 0)
-        nc.gpsimd.memset(kb_win[0:KB_ROW, KB_SPLIT:T].bitcast(I32), 0)
+        nc.vector.memset(kb_win[0:KB_ROW, :].bitcast(I32), 0)
 
         c_rows = cT.rearrange("(p t) n -> p t n", t=4)
 
@@ -105,7 +102,7 @@ def tile_attend_prefer_topk_kernel(tc, qT, k_words, k_scales, cT, kb, offs, offs
         ks_g = tile([P, N], U8, "ks_g")
         k_plane = tile([P, N], U8, "k_plane")
         kw_g = tile([P, N], U32, "kw_g")
-        c_g = [tile([P, 2, HALF], U32, "c_g%d" % h) for h in range(2)]
+        c_g = tile([P, 2 * N], U32, "c_g")
         c_w = [tile([P, HALF, 2, 2], BF16, "c_w0")]
         c_scales = tile([P, N], U8, "c_scales")
         W = HALF // 16
@@ -120,12 +117,17 @@ def tile_attend_prefer_topk_kernel(tc, qT, k_words, k_scales, cT, kb, offs, offs
         def gather_kw(h):
             nc.vector.tensor_copy(out=kw_g[:, h * HALF : (h + 1) * HALF], in_=kw_win[:].bitcast(U32).indirect(list1[:, h * W : (h + 1) * W]))
 
-        def gather_c(u, h):
-            win = c_pair[u][:].rearrange("p n t -> p (n t)").bitcast(U32)
-            nc.vector.tensor_copy(out=c_g[h][:, u, :], in_=win.indirect(list2[:, h * W : (h + 1) * W]))
+        def pair_window(u):
+            return c_pair[u][:].rearrange("p n t -> p (n t)").bitcast(U32)
+
+        def gather_c0():
+            nc.vector.tensor_copy(out=c_g[:].rearrange("p (h u n) -> p h u n", h=2, u=2)[:, :, 0, :], in_=pair_window(0).indirect(list2[:]))
+
+        def gather_c1(h):
+            nc.vector.tensor_copy(out=c_g[:, h * N + HALF : (h + 1) * N], in_=pair_window(1).indirect(list2[:, h * W : (h + 1) * W]))
 
         def weave(h):
-            src = c_g[h][:].rearrange("p u n -> p (u n)").bitcast(BF16).rearrange("p (u n e) -> p n u e", u=2, e=2)
+            src = c_g[:, h * N : (h + 1) * N].bitcast(BF16).rearrange("p (u n e) -> p n u e", u=2, e=2)
             if h == 0:
                 nc.vector.tensor_scalar(out=c_w[h][:], in0=src, scalar1=-1.0, scalar2=None, op0=ALU.mult)
             else:
@@ -137,7 +139,7 @@ def tile_attend_prefer_topk_kernel(tc, qT, k_words, k_scales, cT, kb, offs, offs
             nc.vector.quantize_mx(out=codes[:, a - h * HALF : b - h * HALF].bitcast(FP8X4), scales=c_scales[:, a:b],
                                   in_=c_w[h][:, a - h * HALF : b - h * HALF].rearrange("p n u e -> p (n u e)"))
 
-        acc = [ps.tile([P, b - a], F32, name="acc%d" % i, tag="turn1" if i == 6 else "acc%d" % i) for i, (m, a, b) in enumerate(PIECES)]
+        acc = [ps.tile([P, b - a], F32, name="acc%d" % i, tag="acc%d" % i) for i, (m, a, b) in enumerate(PIECES)]
         logit = [tile([P, b - a], F32, "logit%d" % i) for i, (m, a, b) in enumerate(PIECES)]
         prob = [tile([P, b - a], F32, "prob%d" % i) for i, (m, a, b) in enumerate(PIECES)]
 
@@ -166,18 +168,18 @@ def tile_attend_prefer_topk_kernel(tc, qT, k_words, k_scales, cT, kb, offs, offs
         nc.sync.dma_start(list2[:], offs2)
         load_c(1)
         load_q()
-        load_kw()
         make_identity(nc, ident[:])
         gather_ks()
         place_ks(nc.sync)
+        kw_win = tile([P, T], I32, "kw_win", tag="ks_win")
+        load_kw()
         gather_kb()
         cast_c(0)
-        gather_c(0, 0)
-        gather_c(0, 1)
+        gather_c0()
         cast_c(1)
         turn_kb()
-        gather_c(1, 0)
-        gather_c(1, 1)
+        gather_c1(0)
+        gather_c1(1)
         cast_q()
         weave(0)
         weave(1)
@@ -186,18 +188,18 @@ def tile_attend_prefer_topk_kernel(tc, qT, k_words, k_scales, cT, kb, offs, offs
         quant_c(c_codes[0], 0, HALF)
         kb_all = tile([P, N], F32, "kb_all", tag="q_bf")
         nc.scalar.copy(out=kb_all[:], in_=turn2[:])
-        for i in range(3):
+        for i in range(2):
             mm_c(i, True)
         gather_kw(0)
         gather_kw(1)
-        c_codes.append(tile([P, HALF], U32, "c_codes1", tag="kw_win"))
+        c_codes.append(tile([P, HALF], U32, "c_codes1", tag="ks_win"))
         quant_c(c_codes[1], 256, 384)
         quant_c(c_codes[1], 384, 512)
-        for i in range(3):
+        for i in range(2):
             mm_k(i, False)
-        for i in range(3, len(PIECES)):
+        for i in range(2, len(PIECES)):
             mm_k(i, True)
-        for i in range(3, len(PIECES)):
+        for i in range(2, len(PIECES)):
             mm_c(i, False)
         for i in range(len(PIECES)):
             finish(i, nc.sync)

@@ -19,7 +19,7 @@ HALF = N // 2
 CHUNKS = [(0, 0, 1024, 400), (1, 0, 1024, 400)]
 KB_ROW = 127
 KS_ROW = P - 16
-PIECES = [(0, 0, 256), (1, 0, 256), (0, 256, 384), (1, 256, 384), (0, 384, 512), (1, 384, 512)]
+PIECES = [(0, 0, 256), (1, 0, 256), (0, 256, 384), (0, 384, 512), (1, 256, 384), (1, 384, 512)]
 FLOPS = 2 * 2 * NQ * N * D
 BYTES = 4 * D * NQ + D * T + 16 * T + 4 * D * T2 + 4 * T + 2 * 2 * P * (N // 16) + 4 * NQ * N
 
@@ -141,7 +141,7 @@ def tile_attend_prefer_topk_kernel(tc, qT, k_words, k_scales, cT, kb, offs, offs
 
         acc = [ps.tile([P, b - a], F32, name="acc%d" % i, tag="acc%d" % i) for i, (m, a, b) in enumerate(PIECES)]
         logit = [tile([P, b - a], F32, "logit%d" % i) for i, (m, a, b) in enumerate(PIECES)]
-        prob = [tile([P, b - a], F32, "prob%d" % i) for i, (m, a, b) in enumerate(PIECES)]
+        prob = [tile([P, N], F32, "prob%d" % m) for m in range(2)]
 
         def mm_c(i, start):
             m, a, b = PIECES[i]
@@ -158,8 +158,9 @@ def tile_attend_prefer_topk_kernel(tc, qT, k_words, k_scales, cT, kb, offs, offs
         def finish(i, eng):
             m, a, b = PIECES[i]
             nc.vector.tensor_tensor(out=logit[i][:], in0=acc[i][:], in1=kb_all[:, a:b], op=ALU.add)
-            nc.scalar.activation(out=prob[i][:], in_=logit[i][:], func=ACT.Sigmoid)
-            eng.dma_start(out=out[0, m * P : (m + 1) * P, a:b], in_=prob[i][:])
+            nc.scalar.activation(out=prob[m][:, a:b], in_=logit[i][:], func=ACT.Sigmoid)
+            if b % HALF == 0:
+                eng.dma_start(out=out[0, m * P : (m + 1) * P, b - HALF : b], in_=prob[m][:, b - HALF : b])
 
         nc.sync.dma_start(list1[:], offs)
         load_ks(nc.sync)

@@ -19,7 +19,9 @@ HALF = N // 2
 CHUNKS = [(0, 0, 1024, 400), (1, 0, 1024, 400)]
 KB_ROW = 127
 KS_ROW = P - 16
-PIECES = [(0, 0, 256), (1, 0, 256), (0, 256, 384), (0, 384, 512), (1, 256, 384), (1, 384, 512)]
+PIECES = [(0, 0, 128), (0, 128, 256), (1, 0, 256), (0, 256, 384), (0, 384, 512), (1, 256, 384), (1, 384, 512)]
+FIRST = [i for i, (m, a, b) in enumerate(PIECES) if a < HALF]
+SECOND = [i for i, (m, a, b) in enumerate(PIECES) if a >= HALF]
 FLOPS = 2 * 2 * NQ * N * D
 BYTES = 4 * D * NQ + D * T + 16 * T + 4 * D * T2 + 4 * T + 2 * 2 * P * (N // 16) + 4 * NQ * N
 
@@ -139,7 +141,7 @@ def tile_attend_prefer_topk_kernel(tc, qT, k_words, k_scales, cT, kb, offs, offs
             nc.vector.quantize_mx(out=codes[:, a - h * HALF : b - h * HALF].bitcast(FP8X4), scales=c_scales[:, a:b],
                                   in_=c_w[h][:, a - h * HALF : b - h * HALF].rearrange("p n u e -> p (n u e)"))
 
-        acc = [ps.tile([P, b - a], F32, name="acc%d" % i, tag="acc%d" % i) for i, (m, a, b) in enumerate(PIECES)]
+        acc = [ps.tile([P, b - a], F32, name="acc%d" % i, tag="turn1" if i == 0 else "acc%d" % i) for i, (m, a, b) in enumerate(PIECES)]
         logit = [tile([P, b - a], F32, "logit%d" % i) for i, (m, a, b) in enumerate(PIECES)]
         prob = [tile([P, N], F32, "prob%d" % m) for m in range(2)]
 
@@ -163,7 +165,7 @@ def tile_attend_prefer_topk_kernel(tc, qT, k_words, k_scales, cT, kb, offs, offs
                 eng.dma_start(out=out[0, m * P : (m + 1) * P, b - HALF : b], in_=prob[m][:, b - HALF : b])
 
         nc.sync.dma_start(list1[:], offs)
-        load_ks(nc.sync)
+        load_ks(nc.scalar)
         load_kb(nc.sync)
         load_c(0)
         nc.sync.dma_start(list2[:], offs2)
@@ -189,18 +191,18 @@ def tile_attend_prefer_topk_kernel(tc, qT, k_words, k_scales, cT, kb, offs, offs
         quant_c(c_codes[0], 0, HALF)
         kb_all = tile([P, N], F32, "kb_all", tag="q_bf")
         nc.scalar.copy(out=kb_all[:], in_=turn2[:])
-        for i in range(2):
+        for i in FIRST:
             mm_c(i, True)
         gather_kw(0)
         gather_kw(1)
         c_codes.append(tile([P, HALF], U32, "c_codes1", tag="ks_win"))
         quant_c(c_codes[1], 256, 384)
         quant_c(c_codes[1], 384, 512)
-        for i in range(2):
+        for i in FIRST:
             mm_k(i, False)
-        for i in range(2, len(PIECES)):
+        for i in SECOND:
             mm_k(i, True)
-        for i in range(2, len(PIECES)):
+        for i in SECOND:
             mm_c(i, False)
         for i in range(len(PIECES)):
             finish(i, nc.sync)

@@ -18,7 +18,7 @@ D, NQ, N, T, T2 = 512, 256, 512, 2048, 1024
 HALF = N // 2
 CHUNKS = [(0, 0, 1024, 400), (1, 0, 1024, 400)]
 KB_ROW = 127
-KS_ROW = P - 16
+KS_ROW = 48
 PIECES = [(0, 0, 128), (0, 128, 256), (1, 0, 256), (0, 256, 384), (0, 384, 512), (1, 256, 384), (1, 384, 512)]
 FIRST = [i for i, (m, a, b) in enumerate(PIECES) if a < HALF]
 SECOND = [i for i, (m, a, b) in enumerate(PIECES) if a >= HALF]
@@ -48,7 +48,8 @@ def tile_attend_prefer_topk_kernel(tc, qT, k_words, k_scales, cT, kb, offs, offs
 
         nc.vector.memset(warm[:, 0:1], 0.0)
         nc.scalar.activation(out=warm[:, 1:2], in_=warm[:, 0:1], func=ACT.Sigmoid)
-        nc.gpsimd.memset(ks_win[0:KS_ROW, :].bitcast(I32), 0)
+        nc.vector.memset(ks_win[0:KS_ROW, :].bitcast(I32), 0)
+        nc.vector.memset(ks_win[KS_ROW + 16 : P, :].bitcast(I32), 0)
         nc.vector.memset(kb_win[0:KB_ROW, :].bitcast(I32), 0)
 
         c_rows = cT.rearrange("(p t) n -> p t n", t=4)
@@ -67,7 +68,7 @@ def tile_attend_prefer_topk_kernel(tc, qT, k_words, k_scales, cT, kb, offs, offs
             eng.dma_start(out=kb_win[KB_ROW : KB_ROW + 1, :], in_=kb[0:1, :])
 
         def load_ks(eng):
-            eng.dma_start(out=ks_win[KS_ROW:P, :].bitcast(I32), in_=k_scales[0].bitcast(I32))
+            eng.dma_start(out=ks_win[KS_ROW : KS_ROW + 16, :].bitcast(I32), in_=k_scales[0].bitcast(I32))
 
         q_bf = tile([P, NQ, 4], BF16, "q_bf")
         q_codes = tile([P, NQ], U32, "q_codes")

@@ -14,16 +14,19 @@ ACT = mybir.ActivationFunctionType
 ALU = mybir.AluOpType
 
 P = 128
-D, NQ, N, T, T2 = 512, 256, 512, 2048, 1024
+D, NQ, N = 512, 256, 512
+T, T2 = 2048, 1024
 HALF = N // 2
-CHUNKS = [(0, 0, 1024, 400), (1, 0, 1024, 400)]
-KB_ROW = 127
-KS_ROW = 48
-PIECES = [(0, 0, 128), (0, 128, 256), (1, 0, 256), (0, 256, 384), (0, 384, 512), (1, 256, 384), (1, 384, 512)]
+LIST_COLS = HALF // 16
+SCALE_ROWS = D // 32
+KB_ROW = P - 1
+KS_ROW = P - SCALE_ROWS
+SCALAR_COLS = 400
+PIECES = [(m, a, a + P) for h in range(2) for m in range(2) for a in range(h * HALF, (h + 1) * HALF, P)]
 FIRST = [i for i, (m, a, b) in enumerate(PIECES) if a < HALF]
 SECOND = [i for i, (m, a, b) in enumerate(PIECES) if a >= HALF]
 FLOPS = 2 * 2 * NQ * N * D
-BYTES = 4 * D * NQ + D * T + 16 * T + 4 * D * T2 + 4 * T + 2 * 2 * P * (N // 16) + 4 * NQ * N
+BYTES = 4 * D * NQ + D * T + SCALE_ROWS * T + 4 * D * T2 + 4 * T + 2 * 2 * P * (N // 16) + 4 * NQ * N
 
 
 def tile_attend_prefer_topk_kernel(tc, qT, k_words, k_scales, cT, kb, offs, offs2, out):
@@ -41,169 +44,124 @@ def tile_attend_prefer_topk_kernel(tc, qT, k_words, k_scales, cT, kb, offs, offs
         kb_win = tile([P, T], F32, "kb_win")
         ks_win = tile([P, T], U8, "ks_win")
         q_raw = held.tile([P, 4, NQ], F32, name="q_raw", align_bytes=64, offset=0)
-        c_raw = [tile([P, 2, b - a], F32, "c_raw%d" % i) for i, (u, a, b, s) in enumerate(CHUNKS)]
+        c_raw = [tile([P, 2, T2], F32, "c_raw%d" % u) for u in range(2)]
         c_pair = [tile([P, T2, 2], BF16, "c_pair%d" % u) for u in range(2)]
         warm = tile([P, 2], F32, "warm")
         ident = tile([P, P], F32, "ident")
 
         nc.vector.memset(warm[:, 0:1], 0.0)
         nc.scalar.activation(out=warm[:, 1:2], in_=warm[:, 0:1], func=ACT.Sigmoid)
-        nc.vector.memset(ks_win[0:KS_ROW, :].bitcast(I32), 0)
-        nc.vector.memset(ks_win[KS_ROW + 16 : P, :].bitcast(I32), 0)
+        nc.gpsimd.memset(ks_win[0:KS_ROW, :].bitcast(I32), 0)
         nc.vector.memset(kb_win[0:KB_ROW, :].bitcast(I32), 0)
-
-        c_rows = cT.rearrange("(p t) n -> p t n", t=4)
-
-        def load_c(i):
-            u, a, b, s = CHUNKS[i]
-            nc.sync.dma_start(out=c_raw[i][:], in_=c_rows[:, 2 * u : 2 * u + 2, a:b])
-
-        def load_q():
-            nc.sync.dma_start(out=q_raw[:], in_=qT[0].rearrange("(p t) n -> p t n", t=4))
-
-        def load_kw():
-            nc.sync.dma_start(out=kw_win[:], in_=k_words[0].rearrange("p n t -> p (n t)").bitcast(I32))
-
-        def load_kb(eng):
-            eng.dma_start(out=kb_win[KB_ROW : KB_ROW + 1, :], in_=kb[0:1, :])
-
-        def load_ks(eng):
-            eng.dma_start(out=ks_win[KS_ROW : KS_ROW + 16, :].bitcast(I32), in_=k_scales[0].bitcast(I32))
 
         q_bf = tile([P, NQ, 4], BF16, "q_bf")
         q_codes = tile([P, NQ], U32, "q_codes")
         q_scales = tile([P, NQ], U8, "q_scales")
-
-        def cast_q():
-            nc.scalar.copy(out=q_bf[:].rearrange("p (c i) t -> p c t i", i=4), in_=q_raw[:].rearrange("p t (c i) -> p c t i", i=4))
-
-        def quant_q():
-            nc.vector.quantize_mx(out=q_codes[:].bitcast(FP8X4), scales=q_scales[:], in_=q_bf[:].rearrange("p n t -> p (n t)"))
-
-        def cast_c(i):
-            u, a, b, s = CHUNKS[i]
-            src = c_raw[i][:].rearrange("p t n -> p n t")
-            nc.scalar.activation(out=c_pair[u][:, a : a + s, :], in_=src[:, 0:s, :], func=ACT.Copy)
-            if a + s < b:
-                nc.vector.tensor_copy(out=c_pair[u][:, a + s : b, :], in_=src[:, s : b - a, :])
-
         kb_g = tile([P, N], F32, "kb_g")
         turn1 = ps.tile([P, N], F32, name="turn1", tag="turn1")
-        turn2 = ps.tile([P, N], F32, name="turn2")
-
-        def gather_kb():
-            nc.vector.tensor_copy(out=kb_g[:], in_=kb_win[:].indirect(list1[:]))
-
-        def turn_kb():
-            kb_col = tile([P, 4], F32, "kb_col", tag="c_raw%d" % (len(CHUNKS) - 1))
-            for j in range(4):
-                nc.tensor.transpose(turn1[:, j * P : (j + 1) * P], kb_g[:, j * P : (j + 1) * P], ident[:])
-            nc.scalar.copy(out=kb_col[:], in_=turn1[:, KB_ROW:N:P])
-            for j in range(4):
-                nc.tensor.transpose(turn2[:, j * P : (j + 1) * P], kb_col[:, j : j + 1].to_broadcast([P, P]), ident[:])
-
+        turn2 = ps.tile([P, N], F32, name="turn2", tag="turn2")
         ks_g = tile([P, N], U8, "ks_g")
-        k_plane = tile([P, N], U8, "k_plane")
+        k_scale = tile([P, N], U8, "k_scale")
         kw_g = tile([P, N], U32, "kw_g")
         c_g = tile([P, 2 * N], U32, "c_g")
-        c_w = [tile([P, HALF, 2, 2], BF16, "c_w0")]
-        c_scales = tile([P, N], U8, "c_scales")
-        W = HALF // 16
+        c_woven = [tile([P, HALF, 2, 2], BF16, "c_woven0")]
+        c_scale = tile([P, N], U8, "c_scale")
 
-        def gather_ks():
-            nc.vector.tensor_copy(out=ks_g[:], in_=ks_win[:].indirect(list1[:]))
-
-        def place_ks(eng):
-            for quad in range(4):
-                eng.dma_start(out=k_plane[32 * quad : 32 * quad + 4, :].bitcast(I32), in_=ks_g[KS_ROW + 4 * quad : KS_ROW + 4 * quad + 4, :].bitcast(I32))
-
-        def gather_kw(h):
-            nc.vector.tensor_copy(out=kw_g[:, h * HALF : (h + 1) * HALF], in_=kw_win[:].bitcast(U32).indirect(list1[:, h * W : (h + 1) * W]))
+        def cast_pair(u):
+            src = c_raw[u][:].rearrange("p t n -> p n t")
+            nc.scalar.activation(out=c_pair[u][:, 0:SCALAR_COLS, :], in_=src[:, 0:SCALAR_COLS, :], func=ACT.Copy)
+            nc.vector.tensor_copy(out=c_pair[u][:, SCALAR_COLS:T2, :], in_=src[:, SCALAR_COLS:T2, :])
 
         def pair_window(u):
             return c_pair[u][:].rearrange("p n t -> p (n t)").bitcast(U32)
 
-        def gather_c0():
-            nc.vector.tensor_copy(out=c_g[:].rearrange("p (h u n) -> p h u n", h=2, u=2)[:, :, 0, :], in_=pair_window(0).indirect(list2[:]))
+        def gathered_half(h):
+            return c_g[:, h * N : (h + 1) * N].bitcast(BF16).rearrange("p (u n e) -> p n u e", u=2, e=2)
 
-        def gather_c1(h):
-            nc.vector.tensor_copy(out=c_g[:, h * N + HALF : (h + 1) * N], in_=pair_window(1).indirect(list2[:, h * W : (h + 1) * W]))
-
-        def weave(h):
-            src = c_g[:, h * N : (h + 1) * N].bitcast(BF16).rearrange("p (u n e) -> p n u e", u=2, e=2)
-            if h == 0:
-                nc.vector.tensor_scalar(out=c_w[h][:], in0=src, scalar1=-1.0, scalar2=None, op0=ALU.mult)
-            else:
-                c_w.append(held.tile([P, HALF, 2, 2], BF16, name="c_w1", align_bytes=64, offset=0))
-                nc.scalar.activation(out=c_w[h][:], in_=src, func=ACT.Copy, scale=-1.0)
-
-        def quant_c(codes, a, b):
+        def quantise_c(a, b):
             h = a // HALF
-            nc.vector.quantize_mx(out=codes[:, a - h * HALF : b - h * HALF].bitcast(FP8X4), scales=c_scales[:, a:b],
-                                  in_=c_w[h][:, a - h * HALF : b - h * HALF].rearrange("p n u e -> p (n u e)"))
+            cols = slice(a - h * HALF, b - h * HALF)
+            nc.vector.quantize_mx(out=c_codes[h][:, cols].bitcast(FP8X4), scales=c_scale[:, a:b],
+                                  in_=c_woven[h][:, cols].rearrange("p n u e -> p (n u e)"))
 
-        acc = [ps.tile([P, b - a], F32, name="acc%d" % i, tag="turn1" if i == 0 else "acc%d" % i) for i, (m, a, b) in enumerate(PIECES)]
+        banks = {0: "turn1", len(PIECES) - 1: "turn2"}
+        acc = [ps.tile([P, b - a], F32, name="acc%d" % i, tag=banks.get(i, "acc%d" % i)) for i, (m, a, b) in enumerate(PIECES)]
         logit = [tile([P, b - a], F32, "logit%d" % i) for i, (m, a, b) in enumerate(PIECES)]
         prob = [tile([P, N], F32, "prob%d" % m) for m in range(2)]
 
-        def mm_c(i, start):
+        def multiply(i, words, scale, start):
             m, a, b = PIECES[i]
             rows = slice(m * P, (m + 1) * P)
             nc.tensor.matmul_mx(out=acc[i][:], lhsT=q_codes[:, rows].bitcast(FP8X4), lhsT_scale=q_scales[:, rows],
-                                rhs=c_codes[a // HALF][:, a % HALF : a % HALF + b - a].bitcast(FP8X4), rhs_scale=c_scales[:, a:b], start=start, stop=not start)
+                                rhs=words.bitcast(FP8X4), rhs_scale=scale[:, a:b], start=start, stop=not start)
 
-        def mm_k(i, start):
+        def multiply_c(i, start):
             m, a, b = PIECES[i]
-            rows = slice(m * P, (m + 1) * P)
-            nc.tensor.matmul_mx(out=acc[i][:], lhsT=q_codes[:, rows].bitcast(FP8X4), lhsT_scale=q_scales[:, rows],
-                                rhs=kw_g[:, a:b].bitcast(FP8X4), rhs_scale=k_plane[:, a:b], start=start, stop=not start)
+            multiply(i, c_codes[a // HALF][:, a % HALF : a % HALF + b - a], c_scale, start)
 
-        def finish(i, eng):
+        def multiply_k(i, start):
             m, a, b = PIECES[i]
-            nc.vector.tensor_tensor(out=logit[i][:], in0=acc[i][:], in1=kb_all[:, a:b], op=ALU.add)
-            nc.scalar.activation(out=prob[m][:, a:b], in_=logit[i][:], func=ACT.Sigmoid)
-            if b % HALF == 0:
-                eng.dma_start(out=out[0, m * P : (m + 1) * P, b - HALF : b], in_=prob[m][:, b - HALF : b])
+            multiply(i, kw_g[:, a:b], k_scale, start)
 
+        c_rows = cT.rearrange("(p t) n -> p t n", t=4)
         nc.sync.dma_start(list1[:], offs)
-        load_ks(nc.scalar)
-        load_kb(nc.sync)
-        load_c(0)
+        nc.scalar.dma_start(out=ks_win[KS_ROW : KS_ROW + SCALE_ROWS, :].bitcast(I32), in_=k_scales[0].bitcast(I32))
+        nc.sync.dma_start(out=kb_win[KB_ROW : KB_ROW + 1, :], in_=kb[0:1, :])
+        nc.sync.dma_start(out=c_raw[0][:], in_=c_rows[:, 0:2, :])
         nc.sync.dma_start(list2[:], offs2)
-        load_c(1)
-        load_q()
+        nc.sync.dma_start(out=c_raw[1][:], in_=c_rows[:, 2:4, :])
+        nc.sync.dma_start(out=q_raw[:], in_=qT[0].rearrange("(p t) n -> p t n", t=4))
         make_identity(nc, ident[:])
-        gather_ks()
-        place_ks(nc.sync)
+
+        nc.vector.tensor_copy(out=ks_g[:], in_=ks_win[:].indirect(list1[:]))
+        for quad in range(4):
+            nc.sync.dma_start(out=k_scale[32 * quad : 32 * quad + 4, :].bitcast(I32),
+                              in_=ks_g[KS_ROW + 4 * quad : KS_ROW + 4 * quad + 4, :].bitcast(I32))
         kw_win = tile([P, T], I32, "kw_win", tag="ks_win")
-        load_kw()
-        gather_kb()
-        cast_c(0)
-        gather_c0()
-        cast_c(1)
-        turn_kb()
-        gather_c1(0)
-        gather_c1(1)
-        cast_q()
-        weave(0)
-        weave(1)
-        quant_q()
-        c_codes = [held.tile([P, HALF], U32, name="c_codes0", align_bytes=64, offset=2048)]
-        quant_c(c_codes[0], 0, HALF)
+        nc.sync.dma_start(out=kw_win[:], in_=k_words[0].rearrange("p n t -> p (n t)").bitcast(I32))
+        nc.vector.tensor_copy(out=kb_g[:], in_=kb_win[:].indirect(list1[:]))
+
+        cast_pair(0)
+        nc.vector.tensor_copy(out=c_g[:].rearrange("p (h u n) -> p h u n", h=2, u=2)[:, :, 0, :], in_=pair_window(0).indirect(list2[:]))
+        cast_pair(1)
+
+        kb_col = tile([P, N // P], F32, "kb_col", tag="c_raw1")
+        for j in range(N // P):
+            nc.tensor.transpose(turn1[:, j * P : (j + 1) * P], kb_g[:, j * P : (j + 1) * P], ident[:])
+        nc.scalar.copy(out=kb_col[:], in_=turn1[:, KB_ROW:N:P])
+        for j in range(N // P):
+            nc.tensor.transpose(turn2[:, j * P : (j + 1) * P], kb_col[:, j : j + 1].to_broadcast([P, P]), ident[:])
+
+        for h in range(2):
+            nc.vector.tensor_copy(out=c_g[:, h * N + HALF : (h + 1) * N],
+                                  in_=pair_window(1).indirect(list2[:, h * LIST_COLS : (h + 1) * LIST_COLS]))
+
+        nc.scalar.copy(out=q_bf[:].rearrange("p (c i) t -> p c t i", i=4), in_=q_raw[:].rearrange("p t (c i) -> p c t i", i=4))
+        nc.vector.tensor_scalar(out=c_woven[0][:], in0=gathered_half(0), scalar1=-1.0, scalar2=None, op0=ALU.mult)
+        c_woven.append(held.tile([P, HALF, 2, 2], BF16, name="c_woven1", align_bytes=64, offset=0))
+        nc.scalar.activation(out=c_woven[1][:], in_=gathered_half(1), func=ACT.Copy, scale=-1.0)
+        nc.vector.quantize_mx(out=q_codes[:].bitcast(FP8X4), scales=q_scales[:], in_=q_bf[:].rearrange("p n t -> p (n t)"))
+        c_codes = [held.tile([P, HALF], U32, name="c_codes0", align_bytes=64, offset=HALF * 4 * 2)]
+        quantise_c(0, HALF)
         kb_all = tile([P, N], F32, "kb_all", tag="q_bf")
         nc.scalar.copy(out=kb_all[:], in_=turn2[:])
         for i in FIRST:
-            mm_c(i, True)
-        gather_kw(0)
-        gather_kw(1)
+            multiply_c(i, True)
+
+        for h in range(2):
+            nc.vector.tensor_copy(out=kw_g[:, h * HALF : (h + 1) * HALF],
+                                  in_=kw_win[:].bitcast(U32).indirect(list1[:, h * LIST_COLS : (h + 1) * LIST_COLS]))
         c_codes.append(tile([P, HALF], U32, "c_codes1", tag="ks_win"))
-        quant_c(c_codes[1], 256, 384)
-        quant_c(c_codes[1], 384, 512)
+        for a in range(HALF, N, P):
+            quantise_c(a, a + P)
         for i in FIRST:
-            mm_k(i, False)
+            multiply_k(i, False)
         for i in SECOND:
-            mm_k(i, True)
-        for i in SECOND:
-            mm_c(i, False)
-        for i in range(len(PIECES)):
-            finish(i, nc.sync)
+            multiply_k(i, True)
+            multiply_c(i, False)
+
+        for i, (m, a, b) in enumerate(PIECES):
+            nc.vector.tensor_tensor(out=logit[i][:], in0=acc[i][:], in1=kb_all[:, a:b], op=ALU.add)
+            nc.scalar.activation(out=prob[m][:, a:b], in_=logit[i][:], func=ACT.Sigmoid)
+            if b % HALF == 0:
+                nc.sync.dma_start(out=out[0, m * P : (m + 1) * P, b - HALF : b], in_=prob[m][:, b - HALF : b])

@@ -17,14 +17,11 @@ P = 128
 D, NQ, N = 512, 256, 512
 T, T2 = 2048, 1024
 HALF = N // 2
-LIST_COLS = HALF // 16
 SCALE_ROWS = D // 32
 KB_ROW = P - 1
 KS_ROW = P - SCALE_ROWS
-SCALAR_COLS = 400
+SCALAR_SLOTS = (128, 224, 352, 224)
 PIECES = [(m, a, a + P) for h in range(2) for m in range(2) for a in range(h * HALF, (h + 1) * HALF, P)]
-FIRST = [i for i, (m, a, b) in enumerate(PIECES) if a < HALF]
-SECOND = [i for i, (m, a, b) in enumerate(PIECES) if a >= HALF]
 FLOPS = 2 * 2 * NQ * N * D
 BYTES = 4 * D * NQ + D * T + SCALE_ROWS * T + 4 * D * T2 + 4 * T + 2 * 2 * P * (N // 16) + 4 * NQ * N
 
@@ -33,7 +30,6 @@ def tile_attend_prefer_topk_kernel(tc, qT, k_words, k_scales, cT, kb, offs, offs
     nc = tc.nc
     with ExitStack() as ctx:
         sb = ctx.enter_context(tc.tile_pool(name="sb", bufs=1))
-        held = ctx.enter_context(tc.tile_pool(name="held", bufs=1))
         ps = ctx.enter_context(tc.psum_pool(name="ps", bufs=1))
 
         def tile(shape, dtype, name, tag=None):
@@ -43,9 +39,9 @@ def tile_attend_prefer_topk_kernel(tc, qT, k_words, k_scales, cT, kb, offs, offs
         list2 = tile([P, N // 16], U16, "list2")
         kb_win = tile([P, T], F32, "kb_win")
         ks_win = tile([P, T], U8, "ks_win")
-        q_raw = held.tile([P, 4, NQ], F32, name="q_raw", align_bytes=64, offset=0)
-        c_raw = [tile([P, 2, T2], F32, "c_raw%d" % u) for u in range(2)]
-        c_pair = [tile([P, T2, 2], BF16, "c_pair%d" % u) for u in range(2)]
+        q_raw = tile([P, 4, NQ], F32, "q_raw")
+        c_raw = [tile([P, T2], F32, "c_raw%d" % t) for t in range(4)]
+        c_g = [tile([P, 2, N], BF16, "c_g%d" % u) for u in range(2)]
         warm = tile([P, 2], F32, "warm")
         ident = tile([P, P], F32, "ident")
 
@@ -63,53 +59,35 @@ def tile_attend_prefer_topk_kernel(tc, qT, k_words, k_scales, cT, kb, offs, offs
         ks_g = tile([P, N], U8, "ks_g")
         k_scale = tile([P, N], U8, "k_scale")
         kw_g = tile([P, N], U32, "kw_g")
-        c_g = tile([P, 2 * N], U32, "c_g")
-        c_woven = [tile([P, HALF, 2, 2], BF16, "c_woven0")]
+        c_woven = tile([P, N, 4], BF16, "c_woven")
+        c_codes = tile([P, N], U32, "c_codes")
         c_scale = tile([P, N], U8, "c_scale")
-
-        def cast_pair(u):
-            src = c_raw[u][:].rearrange("p t n -> p n t")
-            nc.scalar.activation(out=c_pair[u][:, 0:SCALAR_COLS, :], in_=src[:, 0:SCALAR_COLS, :], func=ACT.Copy)
-            nc.vector.tensor_copy(out=c_pair[u][:, SCALAR_COLS:T2, :], in_=src[:, SCALAR_COLS:T2, :])
-
-        def pair_window(u):
-            return c_pair[u][:].rearrange("p n t -> p (n t)").bitcast(U32)
-
-        def gathered_half(h):
-            return c_g[:, h * N : (h + 1) * N].bitcast(BF16).rearrange("p (u n e) -> p n u e", u=2, e=2)
-
-        def quantise_c(a, b):
-            h = a // HALF
-            cols = slice(a - h * HALF, b - h * HALF)
-            nc.vector.quantize_mx(out=c_codes[h][:, cols].bitcast(FP8X4), scales=c_scale[:, a:b],
-                                  in_=c_woven[h][:, cols].rearrange("p n u e -> p (n u e)"))
 
         banks = {0: "turn1", len(PIECES) - 1: "turn2"}
         acc = [ps.tile([P, b - a], F32, name="acc%d" % i, tag=banks.get(i, "acc%d" % i)) for i, (m, a, b) in enumerate(PIECES)]
         logit = [tile([P, b - a], F32, "logit%d" % i) for i, (m, a, b) in enumerate(PIECES)]
         prob = [tile([P, N], F32, "prob%d" % m) for m in range(2)]
 
+        def slots(lst, a, b):
+            return lst[:, a // 16 : b // 16]
+
         def multiply(i, words, scale, start):
             m, a, b = PIECES[i]
             rows = slice(m * P, (m + 1) * P)
             nc.tensor.matmul_mx(out=acc[i][:], lhsT=q_codes[:, rows].bitcast(FP8X4), lhsT_scale=q_scales[:, rows],
-                                rhs=words.bitcast(FP8X4), rhs_scale=scale[:, a:b], start=start, stop=not start)
+                                rhs=words[:, a:b].bitcast(FP8X4), rhs_scale=scale[:, a:b], start=start, stop=not start)
 
-        def multiply_c(i, start):
-            m, a, b = PIECES[i]
-            multiply(i, c_codes[a // HALF][:, a % HALF : a % HALF + b - a], c_scale, start)
+        def weave(u, a, b):
+            nc.vector.tensor_scalar(out=c_woven[:, a:b, 2 * u : 2 * u + 2], in0=c_g[u][:, :, a:b].rearrange("p e n -> p n e"),
+                                    scalar1=-1.0, scalar2=None, op0=ALU.mult)
 
-        def multiply_k(i, start):
-            m, a, b = PIECES[i]
-            multiply(i, kw_g[:, a:b], k_scale, start)
-
-        c_rows = cT.rearrange("(p t) n -> p t n", t=4)
+        c_rows = cT.rearrange("(p t) n -> p (t n)", t=4)
         nc.sync.dma_start(list1[:], offs)
         nc.scalar.dma_start(out=ks_win[KS_ROW : KS_ROW + SCALE_ROWS, :].bitcast(I32), in_=k_scales[0].bitcast(I32))
         nc.sync.dma_start(out=kb_win[KB_ROW : KB_ROW + 1, :], in_=kb[0:1, :])
-        nc.sync.dma_start(out=c_raw[0][:], in_=c_rows[:, 0:2, :])
         nc.sync.dma_start(list2[:], offs2)
-        nc.sync.dma_start(out=c_raw[1][:], in_=c_rows[:, 2:4, :])
+        for t in range(4):
+            nc.sync.dma_start(out=c_raw[t][:], in_=c_rows[:, t * T2 : (t + 1) * T2])
         nc.sync.dma_start(out=q_raw[:], in_=qT[0].rearrange("(p t) n -> p t n", t=4))
         make_identity(nc, ident[:])
 
@@ -119,46 +97,45 @@ def tile_attend_prefer_topk_kernel(tc, qT, k_words, k_scales, cT, kb, offs, offs
                               in_=ks_g[KS_ROW + 4 * quad : KS_ROW + 4 * quad + 4, :].bitcast(I32))
         kw_win = tile([P, T], I32, "kw_win", tag="ks_win")
         nc.sync.dma_start(out=kw_win[:], in_=k_words[0].rearrange("p n t -> p (n t)").bitcast(I32))
-        nc.vector.tensor_copy(out=kb_g[:], in_=kb_win[:].indirect(list1[:]))
 
-        cast_pair(0)
-        nc.vector.tensor_copy(out=c_g[:].rearrange("p (h u n) -> p h u n", h=2, u=2)[:, :, 0, :], in_=pair_window(0).indirect(list2[:]))
-        cast_pair(1)
-
-        kb_col = tile([P, N // P], F32, "kb_col", tag="c_raw1")
+        nc.scalar.activation(out=kb_g[:], in_=kb_win[:].indirect(list1[:]), func=ACT.Copy)
         for j in range(N // P):
             nc.tensor.transpose(turn1[:, j * P : (j + 1) * P], kb_g[:, j * P : (j + 1) * P], ident[:])
+        def gather_plane(t):
+            cut = N - SCALAR_SLOTS[t]
+            nc.scalar.activation(out=c_g[t // 2][:, t % 2, cut:N], in_=c_raw[t][:].indirect(slots(list2, cut, N)), func=ACT.Copy)
+            nc.vector.tensor_copy(out=c_g[t // 2][:, t % 2, 0:cut], in_=c_raw[t][:].indirect(slots(list2, 0, cut)))
+
+        gather_plane(0)
+        gather_plane(1)
+        kb_col = tile([P, N // P], F32, "kb_col", tag="c_raw1")
         nc.scalar.copy(out=kb_col[:], in_=turn1[:, KB_ROW:N:P])
         for j in range(N // P):
             nc.tensor.transpose(turn2[:, j * P : (j + 1) * P], kb_col[:, j : j + 1].to_broadcast([P, P]), ident[:])
-
-        for h in range(2):
-            nc.vector.tensor_copy(out=c_g[:, h * N + HALF : (h + 1) * N],
-                                  in_=pair_window(1).indirect(list2[:, h * LIST_COLS : (h + 1) * LIST_COLS]))
-
-        nc.scalar.copy(out=q_bf[:].rearrange("p (c i) t -> p c t i", i=4), in_=q_raw[:].rearrange("p t (c i) -> p c t i", i=4))
-        nc.vector.tensor_scalar(out=c_woven[0][:], in0=gathered_half(0), scalar1=-1.0, scalar2=None, op0=ALU.mult)
-        c_woven.append(held.tile([P, HALF, 2, 2], BF16, name="c_woven1", align_bytes=64, offset=0))
-        nc.scalar.activation(out=c_woven[1][:], in_=gathered_half(1), func=ACT.Copy, scale=-1.0)
-        nc.vector.quantize_mx(out=q_codes[:].bitcast(FP8X4), scales=q_scales[:], in_=q_bf[:].rearrange("p n t -> p (n t)"))
-        c_codes = [held.tile([P, HALF], U32, name="c_codes0", align_bytes=64, offset=HALF * 4 * 2)]
-        quantise_c(0, HALF)
-        kb_all = tile([P, N], F32, "kb_all", tag="q_bf")
+        weave(0, 0, N)
+        gather_plane(2)
+        gather_plane(3)
+        for m in range(2):
+            cols = slice(m * P, (m + 1) * P)
+            nc.scalar.copy(out=q_bf[:, cols].rearrange("p (c i) t -> p c t i", i=4), in_=q_raw[:, :, cols].rearrange("p t (c i) -> p c t i", i=4))
+        kb_all = tile([P, N], F32, "kb_all", tag="q_raw")
         nc.scalar.copy(out=kb_all[:], in_=turn2[:])
-        for i in FIRST:
-            multiply_c(i, True)
-
         for h in range(2):
-            nc.vector.tensor_copy(out=kw_g[:, h * HALF : (h + 1) * HALF],
-                                  in_=kw_win[:].bitcast(U32).indirect(list1[:, h * LIST_COLS : (h + 1) * LIST_COLS]))
-        c_codes.append(tile([P, HALF], U32, "c_codes1", tag="ks_win"))
-        for a in range(HALF, N, P):
-            quantise_c(a, a + P)
-        for i in FIRST:
-            multiply_k(i, False)
-        for i in SECOND:
-            multiply_k(i, True)
-            multiply_c(i, False)
+            weave(1, h * HALF, (h + 1) * HALF)
+        def quantise(codes, scales, values, cols):
+            nc.vector.quantize_mx(out=codes[:, cols].bitcast(FP8X4), scales=scales[:, cols], in_=values[:, cols].rearrange("p n t -> p (n t)"))
+
+        quantise(q_codes, q_scales, q_bf, slice(0, P))
+        for h in range(2):
+            quantise(c_codes, c_scale, c_woven, slice(h * HALF, (h + 1) * HALF))
+        quantise(q_codes, q_scales, q_bf, slice(P, NQ))
+        for i in (0, 1, 4, 5, 2, 3, 6, 7):
+            multiply(i, c_codes, c_scale, True)
+
+        for a in range(0, N, P):
+            nc.vector.tensor_copy(out=kw_g[:, a : a + P], in_=kw_win[:].bitcast(U32).indirect(slots(list1, a, a + P)))
+        for i in (0, 2, 1, 3, 4, 5, 6, 7):
+            multiply(i, kw_g, k_scale, False)
 
         for i, (m, a, b) in enumerate(PIECES):
             nc.vector.tensor_tensor(out=logit[i][:], in0=acc[i][:], in1=kb_all[:, a:b], op=ALU.add)

@@ -20,7 +20,6 @@ HALF = N // 2
 SCALE_ROWS = D // 32
 KB_ROW = P - 1
 KS_ROW = P - SCALE_ROWS
-SCALAR_SLOTS = (128, 224, 352, 224)
 PIECES = [(m, a, a + P) for h in range(2) for m in range(2) for a in range(h * HALF, (h + 1) * HALF, P)]
 FLOPS = 2 * 2 * NQ * N * D
 BYTES = 4 * D * NQ + D * T + SCALE_ROWS * T + 4 * D * T2 + 4 * T + 2 * 2 * P * (N // 16) + 4 * NQ * N
@@ -40,8 +39,8 @@ def tile_attend_prefer_topk_kernel(tc, qT, k_words, k_scales, cT, kb, offs, offs
         kb_win = tile([P, T], F32, "kb_win")
         ks_win = tile([P, T], U8, "ks_win")
         q_raw = tile([P, 4, NQ], F32, "q_raw")
-        c_raw = [tile([P, T2], F32, "c_raw%d" % t) for t in range(4)]
-        c_g = [tile([P, 2, N], BF16, "c_g%d" % u) for u in range(2)]
+        c_raw = [tile([P, 2 * T2], F32, "c_raw%d" % u) for u in range(2)]
+        c_g = [[tile([P, 2, HALF], F32, "c_g%d%d" % (u, h)) for h in range(2)] for u in range(2)]
         warm = tile([P, 2], F32, "warm")
         ident = tile([P, P], F32, "ident")
 
@@ -59,7 +58,7 @@ def tile_attend_prefer_topk_kernel(tc, qT, k_words, k_scales, cT, kb, offs, offs
         ks_g = tile([P, N], U8, "ks_g")
         k_scale = tile([P, N], U8, "k_scale")
         kw_g = tile([P, N], U32, "kw_g")
-        c_woven = tile([P, N, 4], BF16, "c_woven")
+        c_woven = [tile([P, HALF, 4], BF16, "c_woven%d" % h) for h in range(2)]
         c_codes = tile([P, N], U32, "c_codes")
         c_scale = tile([P, N], U8, "c_scale")
 
@@ -77,8 +76,8 @@ def tile_attend_prefer_topk_kernel(tc, qT, k_words, k_scales, cT, kb, offs, offs
             nc.tensor.matmul_mx(out=acc[i][:], lhsT=q_codes[:, rows].bitcast(FP8X4), lhsT_scale=q_scales[:, rows],
                                 rhs=words[:, a:b].bitcast(FP8X4), rhs_scale=scale[:, a:b], start=start, stop=not start)
 
-        def weave(u, a, b):
-            nc.vector.tensor_scalar(out=c_woven[:, a:b, 2 * u : 2 * u + 2], in0=c_g[u][:, :, a:b].rearrange("p e n -> p n e"),
+        def weave(u, h):
+            nc.vector.tensor_scalar(out=c_woven[h][:, :, 2 * u : 2 * u + 2], in0=c_g[u][h][:].rearrange("p e n -> p n e"),
                                     scalar1=-1.0, scalar2=None, op0=ALU.mult)
 
         c_rows = cT.rearrange("(p t) n -> p (t n)", t=4)
@@ -86,8 +85,8 @@ def tile_attend_prefer_topk_kernel(tc, qT, k_words, k_scales, cT, kb, offs, offs
         nc.scalar.dma_start(out=ks_win[KS_ROW : KS_ROW + SCALE_ROWS, :].bitcast(I32), in_=k_scales[0].bitcast(I32))
         nc.sync.dma_start(out=kb_win[KB_ROW : KB_ROW + 1, :], in_=kb[0:1, :])
         nc.sync.dma_start(list2[:], offs2)
-        for t in range(4):
-            nc.sync.dma_start(out=c_raw[t][:], in_=c_rows[:, t * T2 : (t + 1) * T2])
+        for u in range(2):
+            nc.sync.dma_start(out=c_raw[u][:], in_=c_rows[:, 2 * u * T2 : 2 * (u + 1) * T2])
         nc.sync.dma_start(out=q_raw[:], in_=qT[0].rearrange("(p t) n -> p t n", t=4))
         make_identity(nc, ident[:])
 
@@ -101,34 +100,33 @@ def tile_attend_prefer_topk_kernel(tc, qT, k_words, k_scales, cT, kb, offs, offs
         nc.scalar.activation(out=kb_g[:], in_=kb_win[:].indirect(list1[:]), func=ACT.Copy)
         for j in range(N // P):
             nc.tensor.transpose(turn1[:, j * P : (j + 1) * P], kb_g[:, j * P : (j + 1) * P], ident[:])
-        def gather_plane(t):
-            cut = N - SCALAR_SLOTS[t]
-            nc.scalar.activation(out=c_g[t // 2][:, t % 2, cut:N], in_=c_raw[t][:].indirect(slots(list2, cut, N)), func=ACT.Copy)
-            nc.vector.tensor_copy(out=c_g[t // 2][:, t % 2, 0:cut], in_=c_raw[t][:].indirect(slots(list2, 0, cut)))
+        def gather_pair(u):
+            for h in range(2):
+                part = slots(list2, h * HALF, (h + 1) * HALF)
+                nc.scalar.activation(out=c_g[u][h][:, 0, :], in_=c_raw[u][:].indirect(part), func=ACT.Copy)
+                nc.vector.tensor_copy(out=c_g[u][h][:, 1, :], in_=c_raw[u][:, T2 : 2 * T2].indirect(part))
 
-        gather_plane(0)
-        gather_plane(1)
-        kb_col = tile([P, N // P], F32, "kb_col", tag="c_raw1")
+        gather_pair(0)
+        kb_col = tile([P, N // P], F32, "kb_col", tag="c_raw0")
         nc.scalar.copy(out=kb_col[:], in_=turn1[:, KB_ROW:N:P])
         for j in range(N // P):
             nc.tensor.transpose(turn2[:, j * P : (j + 1) * P], kb_col[:, j : j + 1].to_broadcast([P, P]), ident[:])
-        weave(0, 0, N)
-        gather_plane(2)
-        gather_plane(3)
+        for h in range(2):
+            weave(0, h)
+        gather_pair(1)
         for m in range(2):
             cols = slice(m * P, (m + 1) * P)
             nc.scalar.copy(out=q_bf[:, cols].rearrange("p (c i) t -> p c t i", i=4), in_=q_raw[:, :, cols].rearrange("p t (c i) -> p c t i", i=4))
         kb_all = tile([P, N], F32, "kb_all", tag="q_raw")
         nc.scalar.copy(out=kb_all[:], in_=turn2[:])
         for h in range(2):
-            weave(1, h * HALF, (h + 1) * HALF)
-        def quantise(codes, scales, values, cols):
-            nc.vector.quantize_mx(out=codes[:, cols].bitcast(FP8X4), scales=scales[:, cols], in_=values[:, cols].rearrange("p n t -> p (n t)"))
+            weave(1, h)
+        def quantise(codes, scales, cols, values):
+            nc.vector.quantize_mx(out=codes[:, cols].bitcast(FP8X4), scales=scales[:, cols], in_=values.rearrange("p n t -> p (n t)"))
 
-        quantise(q_codes, q_scales, q_bf, slice(0, P))
         for h in range(2):
-            quantise(c_codes, c_scale, c_woven, slice(h * HALF, (h + 1) * HALF))
-        quantise(q_codes, q_scales, q_bf, slice(P, NQ))
+            quantise(c_codes, c_scale, slice(h * HALF, (h + 1) * HALF), c_woven[h][:])
+            quantise(q_codes, q_scales, slice(h * P, (h + 1) * P), q_bf[:, h * P : (h + 1) * P])
         for i in (0, 1, 4, 5, 2, 3, 6, 7):
             multiply(i, c_codes, c_scale, True)
 

@@ -19,7 +19,7 @@ T, T2 = 2048, 1024
 HALF = N // 2
 SCALE_ROWS = D // 32
 KB_ROW = P - 1
-KS_ROW = P - SCALE_ROWS
+KS_ROW = P // 2 - SCALE_ROWS
 PIECES = [(m, a, a + P) for h in range(2) for m in range(2) for a in range(h * HALF, (h + 1) * HALF, P)]
 FLOPS = 2 * 2 * NQ * N * D
 BYTES = 4 * D * NQ + D * T + SCALE_ROWS * T + 4 * D * T2 + 4 * T + 2 * 2 * P * (N // 16) + 4 * NQ * N
@@ -47,6 +47,7 @@ def tile_attend_prefer_topk_kernel(tc, qT, k_words, k_scales, cT, kb, offs, offs
         nc.vector.memset(warm[:, 0:1], 0.0)
         nc.scalar.activation(out=warm[:, 1:2], in_=warm[:, 0:1], func=ACT.Sigmoid)
         nc.gpsimd.memset(ks_win[0:KS_ROW, :].bitcast(I32), 0)
+        nc.vector.memset(ks_win[P // 2 : P, :].bitcast(I32), 0)
         nc.vector.memset(kb_win[0:KB_ROW, :].bitcast(I32), 0)
 
         q_bf = tile([P, NQ, 4], BF16, "q_bf")
@@ -84,9 +85,9 @@ def tile_attend_prefer_topk_kernel(tc, qT, k_words, k_scales, cT, kb, offs, offs
         nc.sync.dma_start(list1[:], offs)
         nc.scalar.dma_start(out=ks_win[KS_ROW : KS_ROW + SCALE_ROWS, :].bitcast(I32), in_=k_scales[0].bitcast(I32))
         nc.sync.dma_start(out=kb_win[KB_ROW : KB_ROW + 1, :], in_=kb[0:1, :])
+        nc.sync.dma_start(out=c_raw[0][:], in_=c_rows[:, 0 : 2 * T2])
         nc.sync.dma_start(list2[:], offs2)
-        for u in range(2):
-            nc.sync.dma_start(out=c_raw[u][:], in_=c_rows[:, 2 * u * T2 : 2 * (u + 1) * T2])
+        nc.sync.dma_start(out=c_raw[1][:], in_=c_rows[:, 2 * T2 : 4 * T2])
         nc.sync.dma_start(out=q_raw[:], in_=qT[0].rearrange("(p t) n -> p t n", t=4))
         make_identity(nc, ident[:])
 

@@ -41,11 +41,8 @@ def tile_attend_prefer_topk_kernel(tc, qT, k_words, k_scales, cT, kb, offs, offs
         q_raw = tile([P, 4, NQ], F32, "q_raw")
         c_raw = [tile([P, 2 * T2], F32, "c_raw%d" % u) for u in range(2)]
         c_g = [[tile([P, 2, HALF], F32, "c_g%d%d" % (u, h)) for h in range(2)] for u in range(2)]
-        warm = tile([P, 2], F32, "warm")
         ident = tile([P, P], F32, "ident")
 
-        nc.vector.memset(warm[:, 0:1], 0.0)
-        nc.scalar.activation(out=warm[:, 1:2], in_=warm[:, 0:1], func=ACT.Sigmoid)
         nc.gpsimd.memset(ks_win[0:KS_ROW, :].bitcast(I32), 0)
         nc.vector.memset(ks_win[P // 2 : P, :].bitcast(I32), 0)
         nc.vector.memset(kb_win[0:KB_ROW, :].bitcast(I32), 0)

from contextlib import ExitStack

import concourse.mybir as mybir
from concourse.masks import make_identity

F32 = mybir.dt.float32
BF16 = mybir.dt.bfloat16
I32 = mybir.dt.int32
U32 = mybir.dt.uint32
U16 = mybir.dt.uint16
U8 = mybir.dt.uint8
FP8X4 = mybir.dt.float8_e4m3fn_x4
ACT = mybir.ActivationFunctionType
ALU = mybir.AluOpType

P = 128
D, NQ, N = 512, 256, 512
T, T2 = 2048, 1024
HALF = N // 2
SCALE_ROWS = D // 32
KB_ROW = P - 1
KS_ROW = P // 2 - SCALE_ROWS
PIECES = [(m, a, a + P) for h in range(2) for m in range(2) for a in range(h * HALF, (h + 1) * HALF, P)]
FLOPS = 2 * 2 * NQ * N * D
BYTES = 4 * D * NQ + D * T + SCALE_ROWS * T + 4 * D * T2 + 4 * T + 2 * 2 * P * (N // 16) + 4 * NQ * N


def tile_attend_prefer_topk_kernel(tc, qT, k_words, k_scales, cT, kb, offs, offs2, out):
    nc = tc.nc
    with ExitStack() as ctx:
        sb = ctx.enter_context(tc.tile_pool(name="sb", bufs=1))
        ps = ctx.enter_context(tc.psum_pool(name="ps", bufs=1))

        def tile(shape, dtype, name, tag=None):
            return sb.tile(shape, dtype, name=name, tag=tag or name, align_bytes=64)

        list1 = tile([P, N // 16], U16, "list1")
        list2 = tile([P, N // 16], U16, "list2")
        kb_win = tile([P, T], F32, "kb_win")
        ks_win = tile([P, T], U8, "ks_win")
        q_raw = tile([P, 4, NQ], F32, "q_raw")
        c_raw = [tile([P, 2 * T2], F32, "c_raw%d" % u) for u in range(2)]
        c_g = [[tile([P, 2, HALF], F32, "c_g%d%d" % (u, h)) for h in range(2)] for u in range(2)]
        ident = tile([P, P], F32, "ident")

        nc.gpsimd.memset(ks_win[0:KS_ROW, :].bitcast(I32), 0)
        nc.vector.memset(ks_win[P // 2 : P, :].bitcast(I32), 0)
        nc.vector.memset(kb_win[0:KB_ROW, :].bitcast(I32), 0)

        q_bf = tile([P, NQ, 4], BF16, "q_bf")
        q_codes = tile([P, NQ], U32, "q_codes")
        q_scales = tile([P, NQ], U8, "q_scales")
        kb_g = tile([P, N], F32, "kb_g")
        turn1 = ps.tile([P, N], F32, name="turn1", tag="turn1")
        turn2 = ps.tile([P, N], F32, name="turn2", tag="turn2")
        ks_g = tile([P, N], U8, "ks_g")
        k_scale = tile([P, N], U8, "k_scale")
        kw_g = tile([P, N], U32, "kw_g")
        c_woven = [tile([P, HALF, 4], BF16, "c_woven%d" % h) for h in range(2)]
        c_codes = tile([P, N], U32, "c_codes")
        c_scale = tile([P, N], U8, "c_scale")

        banks = {0: "turn1", len(PIECES) - 1: "turn2"}
        acc = [ps.tile([P, b - a], F32, name="acc%d" % i, tag=banks.get(i, "acc%d" % i)) for i, (m, a, b) in enumerate(PIECES)]
        logit = [tile([P, b - a], F32, "logit%d" % i) for i, (m, a, b) in enumerate(PIECES)]
        prob = [tile([P, N], F32, "prob%d" % m) for m in range(2)]

        def slots(lst, a, b):
            return lst[:, a // 16 : b // 16]

        def multiply(i, words, scale, start):
            m, a, b = PIECES[i]
            rows = slice(m * P, (m + 1) * P)
            nc.tensor.matmul_mx(out=acc[i][:], lhsT=q_codes[:, rows].bitcast(FP8X4), lhsT_scale=q_scales[:, rows],
                                rhs=words[:, a:b].bitcast(FP8X4), rhs_scale=scale[:, a:b], start=start, stop=not start)

        def weave(u, h):
            nc.vector.tensor_scalar(out=c_woven[h][:, :, 2 * u : 2 * u + 2], in0=c_g[u][h][:].rearrange("p e n -> p n e"),
                                    scalar1=-1.0, scalar2=None, op0=ALU.mult)

        c_rows = cT.rearrange("(p t) n -> p (t n)", t=4)
        nc.sync.dma_start(list1[:], offs)
        nc.scalar.dma_start(out=ks_win[KS_ROW : KS_ROW + SCALE_ROWS, :].bitcast(I32), in_=k_scales[0].bitcast(I32))
        nc.sync.dma_start(out=kb_win[KB_ROW : KB_ROW + 1, :], in_=kb[0:1, :])
        nc.sync.dma_start(out=c_raw[0][:], in_=c_rows[:, 0 : 2 * T2])
        nc.sync.dma_start(list2[:], offs2)
        nc.sync.dma_start(out=c_raw[1][:], in_=c_rows[:, 2 * T2 : 4 * T2])
        nc.sync.dma_start(out=q_raw[:], in_=qT[0].rearrange("(p t) n -> p t n", t=4))
        make_identity(nc, ident[:])

        nc.vector.tensor_copy(out=ks_g[:], in_=ks_win[:].indirect(list1[:]))
        for quad in range(4):
            nc.sync.dma_start(out=k_scale[32 * quad : 32 * quad + 4, :].bitcast(I32),
                              in_=ks_g[KS_ROW + 4 * quad : KS_ROW + 4 * quad + 4, :].bitcast(I32))
        kw_win = tile([P, T], I32, "kw_win", tag="ks_win")
        nc.sync.dma_start(out=kw_win[:], in_=k_words[0].rearrange("p n t -> p (n t)").bitcast(I32))

        nc.scalar.activation(out=kb_g[:], in_=kb_win[:].indirect(list1[:]), func=ACT.Copy)
        for j in range(N // P):
            nc.tensor.transpose(turn1[:, j * P : (j + 1) * P], kb_g[:, j * P : (j + 1) * P], ident[:])
        def gather_pair(u):
            for h in range(2):
                part = slots(list2, h * HALF, (h + 1) * HALF)
                nc.scalar.activation(out=c_g[u][h][:, 0, :], in_=c_raw[u][:].indirect(part), func=ACT.Copy)
                nc.vector.tensor_copy(out=c_g[u][h][:, 1, :], in_=c_raw[u][:, T2 : 2 * T2].indirect(part))

        gather_pair(0)
        kb_col = tile([P, N // P], F32, "kb_col", tag="c_raw0")
        nc.scalar.copy(out=kb_col[:], in_=turn1[:, KB_ROW:N:P])
        for j in range(N // P):
            nc.tensor.transpose(turn2[:, j * P : (j + 1) * P], kb_col[:, j : j + 1].to_broadcast([P, P]), ident[:])
        for h in range(2):
            weave(0, h)
        gather_pair(1)
        for m in range(2):
            cols = slice(m * P, (m + 1) * P)
            nc.scalar.copy(out=q_bf[:, cols].rearrange("p (c i) t -> p c t i", i=4), in_=q_raw[:, :, cols].rearrange("p t (c i) -> p c t i", i=4))
        kb_all = tile([P, N], F32, "kb_all", tag="q_raw")
        nc.scalar.copy(out=kb_all[:], in_=turn2[:])
        for h in range(2):
            weave(1, h)
        def quantise(codes, scales, cols, values):
            nc.vector.quantize_mx(out=codes[:, cols].bitcast(FP8X4), scales=scales[:, cols], in_=values.rearrange("p n t -> p (n t)"))

        for h in range(2):
            quantise(c_codes, c_scale, slice(h * HALF, (h + 1) * HALF), c_woven[h][:])
            quantise(q_codes, q_scales, slice(h * P, (h + 1) * P), q_bf[:, h * P : (h + 1) * P])
        for i in (0, 1, 4, 5, 2, 3, 6, 7):
            multiply(i, c_codes, c_scale, True)

        for a in range(0, N, P):
            nc.vector.tensor_copy(out=kw_g[:, a : a + P], in_=kw_win[:].bitcast(U32).indirect(slots(list1, a, a + P)))
        for i in (0, 2, 1, 3, 4, 5, 6, 7):
            multiply(i, kw_g, k_scale, False)

        for i, (m, a, b) in enumerate(PIECES):
            nc.vector.tensor_tensor(out=logit[i][:], in0=acc[i][:], in1=kb_all[:, a:b], op=ALU.add)
            nc.scalar.activation(out=prob[m][:, a:b], in_=logit[i][:], func=ACT.Sigmoid)
            if b % HALF == 0:
                nc.sync.dma_start(out=out[0, m * P : (m + 1) * P, b - HALF : b], in_=prob[m][:, b - HALF : b])
